import numpy as np
import ml_dtypes


def mxq(x, axis, fmt="e4m3"):
    dtype, down = {"e4m3": (ml_dtypes.float8_e4m3fn, 7), "e5m2": (ml_dtypes.float8_e5m2, 14)}[fmt]
    v = np.moveaxis(np.asarray(x, np.float32).astype(ml_dtypes.bfloat16).astype(np.float64), axis, -1)
    blocks = v.reshape(v.shape[:-1] + (-1, 32))
    amax = np.abs(blocks).max(-1, keepdims=True)
    byte = np.maximum(np.where(amax > 0, np.frexp(amax)[1] - 1 + 127, 0) - down, 1)
    scale = np.exp2(byte - 127.0)
    codes = (blocks / scale).astype(np.float32).astype(dtype).astype(np.float64)
    return np.moveaxis((codes * scale).reshape(v.shape), -1, axis)


WIDE = False


def mx_kscale(k):
    if not WIDE:
        return np.ones(k)
    levels = np.array([10, -10, 5, -5, 0])
    if k % 512:
        return np.exp2(np.random.permutation(np.resize(levels, k // 32))).repeat(32)
    a = np.empty((k // 512, 16))
    for p in range(k // 512):
        a[p, :8] = np.random.permutation(np.resize(levels, 8))
        for g in range(8):
            far = levels[np.abs(levels - a[p, g]) >= 10]
            a[p, g + 8] = far[np.random.randint(len(far))]
    return np.exp2(a.ravel()).repeat(32)


def f64(x):
    return np.asarray(x).astype(np.float64)


def striped(idx):
    return np.tile(idx.reshape(-1, 16).T, (8, 1)).astype(np.uint16)


def unstriped(offs):
    return offs[:16].T.reshape(-1).astype(np.int64)


E2M1 = np.array([0.0, 0.5, 1.0, 1.5, 2.0, 3.0, 4.0, 6.0, -0.0, -0.5, -1.0, -1.5, -2.0, -3.0, -4.0, -6.0])


def pack_weight(w, fmt):
    k, n = w.shape
    w = f64(np.asarray(w, np.float32).astype(ml_dtypes.bfloat16)).reshape(k // 32, 32, n)
    amax = np.abs(w).max(1)
    if fmt == "e4m3":
        byte = np.frexp(amax)[1] - 1 + 127 - 7
    else:
        mant, ex = np.frexp(amax / 6.0)
        byte = np.where(mant > 0.5, ex, ex - 1) + 127
    byte = np.clip(np.where(amax > 0, byte, 1), 1, 254)
    scaled = (w * np.exp2(127.0 - byte)[:, None, :]).reshape(k, n).astype(np.float32)
    by_word = np.ascontiguousarray(scaled.reshape(k // 512, 128, 4, n).transpose(0, 1, 3, 2))
    if fmt == "e4m3":
        words = by_word.astype(ml_dtypes.float8_e4m3fn).view(np.uint8)
    else:
        c = by_word.astype(ml_dtypes.float4_e2m1fn).view(np.uint8) & 0xF
        words = (c[..., 0::2] | (c[..., 1::2] << 4)).reshape(k // 512, 128, 2 * n)
    return np.ascontiguousarray(words), np.ascontiguousarray(byte.astype(np.uint8).reshape(k // 512, 16, n))


def unpack_weight(words, scales, fmt):
    g, _, n = scales.shape
    words = np.ascontiguousarray(words).reshape(g, 128, n, -1)
    if fmt == "e4m3":
        vals = words.view(ml_dtypes.float8_e4m3fn).astype(np.float64)
    else:
        nib = np.empty((g, 128, n, 4), np.uint8)
        nib[..., 0::2] = words & 0xF
        nib[..., 1::2] = words >> 4
        vals = E2M1[nib]
    vals = vals * np.repeat(np.exp2(scales.astype(np.float64) - 127.0), 8, axis=1)[..., None]
    return vals.transpose(0, 1, 3, 2).reshape(g * 512, n)


def d_sigmoid(v):
    s = 1.0 / (1.0 + np.exp(-np.maximum(v, -700.0)))
    return s * (1.0 - s)


def sigmoid(v):
    return 1.0 / (1.0 + np.exp(-np.maximum(v, -700.0)))


K, T, E, C, H, N = 512, 512, 4, 128, 512, 512


def by_expert(wq, xq):
    return np.concatenate([wq[e].T @ xq[:, e * C:(e + 1) * C] for e in range(E)], axis=1)


def setup_inputs():
    n = np.random.standard_normal
    s = mx_kscale(K)
    v = mx_kscale(N)
    u = mx_kscale(H)
    slot_token = np.random.permutation(T)[:E * C]
    w_slot = np.random.uniform(0.2, 1.0, E * C)
    x = pack_weight(n((K, T)) * s[:, None], "e4m3")
    dy = pack_weight(n((N, T)) * v[:, None], "e4m3")
    m1 = n((E, K, H))
    m3 = n((E, K, H))
    w1 = [pack_weight(m, "e2m1") for m in m1 / np.sqrt(K) / s[None, :, None]]
    w3 = [pack_weight(m, "e2m1") for m in m3 / np.sqrt(K) / s[None, :, None]]
    w2t = [pack_weight(m, "e2m1") for m in n((E, N, H)) / np.sqrt(N) / v[None, :, None] * u]
    w1t = [pack_weight(m, "e2m1") for m in m1.transpose(0, 2, 1) / np.sqrt(H) / u[None, :, None]]
    w3t = [pack_weight(m, "e2m1") for m in m3.transpose(0, 2, 1) / np.sqrt(H) / u[None, :, None]]
    return {
        "x_words": x[0],
        "x_scales": x[1],
        "dy_words": dy[0],
        "dy_scales": dy[1],
        "w1_words": np.stack([m[0] for m in w1]),
        "w1_scales": np.stack([m[1] for m in w1]),
        "w3_words": np.stack([m[0] for m in w3]),
        "w3_scales": np.stack([m[1] for m in w3]),
        "w2t_words": np.stack([m[0] for m in w2t]),
        "w2t_scales": np.stack([m[1] for m in w2t]),
        "w1t_words": np.stack([m[0] for m in w1t]),
        "w1t_scales": np.stack([m[1] for m in w1t]),
        "w3t_words": np.stack([m[0] for m in w3t]),
        "w3t_scales": np.stack([m[1] for m in w3t]),
        "gate": (np.tile(w_slot, (128, 1))).astype(np.float32),
        "offs": striped(slot_token),
    }


def reference(x_words, x_scales, dy_words, dy_scales, w1_words, w1_scales, w3_words, w3_scales, w2t_words, w2t_scales, w1t_words, w1t_scales, w3t_words, w3t_scales, gate, offs):
    w1 = np.stack([unpack_weight(w1_words[e], w1_scales[e], "e2m1") for e in range(E)])
    w3 = np.stack([unpack_weight(w3_words[e], w3_scales[e], "e2m1") for e in range(E)])
    w2t = np.stack([unpack_weight(w2t_words[e], w2t_scales[e], "e2m1") for e in range(E)])
    w1t = np.stack([unpack_weight(w1t_words[e], w1t_scales[e], "e2m1") for e in range(E)])
    w3t = np.stack([unpack_weight(w3t_words[e], w3t_scales[e], "e2m1") for e in range(E)])
    idx = unstriped(offs)
    xq = unpack_weight(x_words, x_scales, "e4m3")[:, idx]
    gq = unpack_weight(dy_words, dy_scales, "e4m3")[:, idx]
    dh = f64(gate[:1]) * by_expert(w2t, gq)
    a1, a3 = by_expert(w1, xq), by_expert(w3, xq)
    dx = by_expert(w1t, mxq(dh * a3 * d_sigmoid(a1), 0, "e4m3")) + by_expert(w3t, mxq(dh * sigmoid(a1), 0, "e4m3"))
    out = np.zeros((K, T))
    out[:, idx] = dx
    return out

@@ -1,0 +1,218 @@
+from contextlib import ExitStack
+
+import concourse.mybir as mybir
+from concourse.masks import make_identity
+
+K, T, E, C, H, N = 512, 512, 4, 128, 512, 512
+FLOPS = 5 * 2 * 512 * 512 * 512
+
+F32 = mybir.dt.float32
+BF16 = mybir.dt.bfloat16
+I32 = mybir.dt.int32
+U32 = mybir.dt.uint32
+U16 = mybir.dt.uint16
+U8 = mybir.dt.uint8
+FP8X4 = mybir.dt.float8_e4m3fn_x4
+FP4X4 = mybir.dt.float4_e2m1fn_x4
+MULT = mybir.AluOpType.mult
+SIGMOID = mybir.ActivationFunctionType.Sigmoid
+COPY = mybir.ActivationFunctionType.Copy
+
+P = 128
+
+
+def tile_moe_rec_glu_sigmoid_kernel(
+    tc, x_words, x_scales, dy_words, dy_scales, w1_words, w1_scales, w3_words, w3_scales,
+    w2t_words, w2t_scales, w1t_words, w1t_scales, w3t_words, w3t_scales, gate, offs, out,
+):
+    nc = tc.nc
+    with ExitStack() as ctx:
+        keep = ctx.enter_context(tc.tile_pool(name="keep", bufs=1))
+        work = ctx.enter_context(tc.tile_pool(name="work", bufs=4))
+        psum = ctx.enter_context(tc.psum_pool(name="psum", bufs=1))
+
+        offsets = keep.tile([P, T // 16], U16, name="offsets")
+        x_win = keep.tile([P, T], I32, name="x_win", align_bytes=64)
+        dy_win = keep.tile([P, T], I32, name="dy_win", align_bytes=64)
+        xs_win = keep.tile([P, T], U8, name="xs_win", align_bytes=64)
+        dys_win = keep.tile([P, T], U8, name="dys_win", align_bytes=64)
+        names = ("w1", "w2t", "w3", "w1t", "w3t")
+        words_in = {"w1": w1_words, "w2t": w2t_words, "w3": w3_words, "w1t": w1t_words, "w3t": w3t_words}
+        scales_in = {"w1": w1_scales, "w2t": w2t_scales, "w3": w3_scales, "w1t": w1t_scales, "w3t": w3t_scales}
+        w = {n: keep.tile([P, E, 1024], U8, name=n + "_w", align_bytes=64) for n in names}
+        ws = {n: keep.tile([P, E, 512], U8, name=n + "_s", align_bytes=64) for n in names}
+        g_col = keep.tile([P, E], F32, name="g_col")
+        ident = keep.tile([P, P], F32, name="ident")
+        warm_in = keep.tile([P, 1], F32, name="warm_in")
+        warm_out = keep.tile([P, 1], F32, name="warm_out")
+
+        def zero(tile):
+            nc.vector.memset(tile.bitcast(I32), 0)
+
+        def zero_plane(n):
+            zero(ws[n][:].rearrange("p e c -> p (e c)"))
+
+        zero(xs_win[:])
+        zero_plane("w1")
+        nc.vector.memset(warm_in[:], 0.0)
+        nc.scalar.activation(warm_out[:], warm_in[:], SIGMOID)
+        zero(dys_win[:])
+        for n in ("w2t", "w3", "w1t", "w3t"):
+            zero_plane(n)
+
+        def load_token_scales(tile, src):
+            for r in range(4):
+                nc.sync.dma_start(tile[r:P:32, :].bitcast(I32), src[0, r:16:4, :].bitcast(I32))
+
+        def load_weight_scales(n):
+            for r in range(4):
+                nc.sync.dma_start(
+                    ws[n][r:P:32, :, :].bitcast(I32),
+                    scales_in[n][:, 0, r:16:4, :].rearrange("e b c -> b e c").bitcast(I32),
+                )
+
+        def load_words(queue, n, lo, hi):
+            queue.dma_start(
+                w[n][:, lo:hi, :].bitcast(I32), words_in[n][lo:hi, 0, :, :].rearrange("e p c -> p e c").bitcast(I32)
+            )
+
+        def load_gate():
+            with nc.allow_non_contiguous_dma(reason="one gate value a partition and expert"):
+                nc.sync.dma_start(g_col[:], gate[0, :].rearrange("(e u) -> u e", e=E))
+
+        for n in ("w1", "w2t", "w3"):
+            load_words(nc.gpsimd, n, 0, 2)
+        make_identity(nc, ident[:])
+
+        nc.sync.dma_start(offsets[:], offs)
+        nc.sync.dma_start(x_win[:], x_words[0].rearrange("p t d -> p (t d)").bitcast(I32))
+        load_token_scales(xs_win, x_scales)
+        load_weight_scales("w1")
+        nc.sync.dma_start(dy_win[:], dy_words[0].rearrange("p t d -> p (t d)").bitcast(I32))
+        load_token_scales(dys_win, dy_scales)
+        load_weight_scales("w2t")
+        load_gate()
+        for n in ("w3", "w1t", "w3t"):
+            load_weight_scales(n)
+        for n in ("w1t", "w3t"):
+            load_words(nc.sync, n, 0, 2)
+        for n in ("w1", "w2t", "w3", "w1t", "w3t"):
+            load_words(nc.sync, n, 2, 4)
+
+        xg = keep.tile([P, T], U32, name="xg", align_bytes=64)
+        dyg = keep.tile([P, T], U32, name="dyg", align_bytes=64)
+        xsg = keep.tile([P, T], U8, name="xsg", align_bytes=64)
+        dysg = keep.tile([P, T], U8, name="dysg", align_bytes=64)
+
+        def gather_x(lo, hi):
+            part = offsets[:, lo // 16 : hi // 16]
+            nc.vector.tensor_copy(xg[:, lo:hi], x_win[:].bitcast(U32).indirect(part))
+            nc.vector.tensor_copy(xsg[:, lo:hi], xs_win[:].indirect(part))
+
+        def gather_dy(lo, hi):
+            part = offsets[:, lo // 16 : hi // 16]
+            nc.vector.tensor_copy(dyg[:, lo:hi], dy_win[:].bitcast(U32).indirect(part))
+            nc.vector.tensor_copy(dysg[:, lo:hi], dys_win[:].indirect(part))
+
+        def gather(lo, hi):
+            gather_x(lo, hi)
+            gather_dy(lo, hi)
+
+        dx_sb = keep.tile([P, 4, T], F32, name="dx_sb")
+        out_sb = [keep.tile([P, T], F32, name="out_sb%d" % kt) for kt in range(4)]
+        state = {}
+
+        def order(ap):
+            return ap.rearrange("p (m u v) -> p u m v", u=2, v=2)
+
+        def as_order(ap):
+            return ap.rearrange("p (u m v) -> p u m v", u=2, v=2)
+
+        def planes(ap):
+            return ap.rearrange("p (m t) -> p t m", t=4)
+
+        def as_planes(ap):
+            return ap.rearrange("p (t m) -> p t m", t=4)
+
+        def first_product(e, tag, codes, code_scales, n, bufs):
+            bank = psum.tile([P, H], F32, name=tag, bufs=bufs)
+            cols = slice(e * C, (e + 1) * C)
+            nc.tensor.matmul_mx(
+                out=bank[:], lhsT=codes[:, cols].bitcast(FP8X4), lhsT_scale=code_scales[:, cols],
+                rhs=w[n][:, e, :].bitcast(FP4X4), rhs_scale=ws[n][:, e, :], start=True, stop=True,
+            )
+            return bank
+
+        def stage_a(e):
+            a1 = first_product(e, "a1", xg, xsg, "w1", 1)
+            dh = first_product(e, "dh", dyg, dysg, "w2t", 2)
+            a3 = first_product(e, "a3", xg, xsg, "w3", 2)
+            s = work.tile([P, H], F32, name="s")
+            sn = work.tile([P, H], F32, name="sn")
+            nc.scalar.activation(as_planes(s[:]), planes(a1[:]), SIGMOID)
+            nc.scalar.activation(as_order(sn[:]), order(a1[:]), SIGMOID, scale=-1.0)
+            da3 = work.tile([P, H], F32, name="da3")
+            nc.vector.scalar_tensor_tensor(as_planes(da3[:]), planes(dh[:]), g_col[:, e : e + 1], as_planes(s[:]), MULT, MULT)
+            u = work.tile([P, H], F32, name="u")
+            nc.vector.tensor_tensor(as_order(u[:]), order(a3[:]), as_order(sn[:]), MULT)
+            state[e] = (da3, u)
+
+        def stage_b(e):
+            da3, u = state[e]
+            da1 = work.tile([P, H], BF16, name="da1")
+            nc.vector.tensor_tensor(
+                as_order(da1[:]), da3[:].rearrange("p (u v m) -> p u m v", u=2, v=2), as_order(u[:]), MULT
+            )
+            tr3 = psum.tile([P, 4, C], F32, name="tr3")
+            tr1 = psum.tile([P, 2, C], F32, name="tr1")
+            for t in range(4):
+                nc.tensor.transpose(tr3[:, t, :], da3[:, t * P : (t + 1) * P], ident[:])
+            for h in range(2):
+                nc.tensor.transpose(tr1[:, h, :], da1[:].bitcast(F32)[:, h * P : (h + 1) * P], ident[:])
+            q_in = work.tile([P, 2, C * 4], BF16, name="q_in", align_bytes=64)
+            nc.scalar.activation(q_in[:, 1, :].rearrange("p (c t) -> p c t", t=4), tr3[:].rearrange("p t c -> p c t"), COPY)
+            nc.scalar.copy(q_in[:, 0, :].bitcast(F32).rearrange("p (c h) -> p c h", h=2), tr1[:].rearrange("p h c -> p c h"))
+            state[e] = q_in
+
+        def stage_c(e):
+            q_in = state[e]
+            codes = work.tile([P, 2 * C], U32, name="codes", align_bytes=64)
+            code_scales = work.tile([P, 2 * C], U8, name="code_scales", align_bytes=64)
+            nc.vector.quantize_mx(out=codes[:].bitcast(FP8X4), scales=code_scales[:], in_=q_in[:].rearrange("p a c -> p (a c)"))
+            dx = psum.tile([P, 4, C], F32, name="dx")
+            for kt in range(4):
+                for j, n in enumerate(("w1t", "w3t")):
+                    nc.tensor.matmul_mx(
+                        out=dx[:, kt, :],
+                        lhsT=w[n][:, e, 2 * P * kt : 2 * P * (kt + 1)].bitcast(FP4X4),
+                        lhsT_scale=ws[n][:, e, P * kt : P * (kt + 1)],
+                        rhs=codes[:, j * C : (j + 1) * C].bitcast(FP8X4),
+                        rhs_scale=code_scales[:, j * C : (j + 1) * C],
+                        start=(j == 0), stop=(j == 1),
+                    )
+            nc.scalar.copy(dx_sb[:, :, e * C : (e + 1) * C], dx[:])
+
+        def scatter(kt, lo, hi):
+            nc.vector.tensor_copy(out_sb[kt][:].indirect(offsets[:, lo // 16 : hi // 16]), dx_sb[:, kt, lo:hi])
+
+        gather(0, 256)
+        gather(256, 512)
+        stage_a(0)
+        stage_a(1)
+        stage_b(0)
+        stage_a(2)
+        stage_b(1)
+        stage_c(0)
+        stage_a(3)
+        stage_b(2)
+        stage_c(1)
+        for kt in range(4):
+            scatter(kt, 0, 128)
+        stage_b(3)
+        stage_c(2)
+        for kt in range(4):
+            scatter(kt, 128, 256)
+        stage_c(3)
+        for kt in range(4):
+            scatter(kt, 256, 512)
+            nc.sync.dma_start(out[kt * P : (kt + 1) * P, :], out_sb[kt][:])

@@ -57,7 +57,7 @@ def tile_moe_rec_glu_sigmoid_kernel(
         nc.vector.memset(warm_in[:], 0.0)
         nc.scalar.activation(warm_out[:], warm_in[:], SIGMOID)
         zero(dys_win[:])
-        for n in ("w2t", "w3", "w1t", "w3t"):
+        for n in ("w2t", "w3"):
             zero_plane(n)
 
         def load_token_scales(tile, src):
@@ -80,24 +80,22 @@ def tile_moe_rec_glu_sigmoid_kernel(
             with nc.allow_non_contiguous_dma(reason="one gate value a partition and expert"):
                 nc.sync.dma_start(g_col[:], gate[0, :].rearrange("(e u) -> u e", e=E))
 
-        for n in ("w1", "w2t", "w3"):
-            load_words(nc.gpsimd, n, 0, 2)
+        for n in ("w1t", "w3t"):
+            zero_plane(n)
+        for n in ("w1", "w2t", "w3", "w1t"):
+            load_words(nc.gpsimd, n, 0, 4)
         make_identity(nc, ident[:])
+        load_words(nc.gpsimd, "w3t", 0, 4)
 
         nc.sync.dma_start(offsets[:], offs)
         nc.sync.dma_start(x_win[:], x_words[0].rearrange("p t d -> p (t d)").bitcast(I32))
+        nc.sync.dma_start(dy_win[:], dy_words[0].rearrange("p t d -> p (t d)").bitcast(I32))
+        load_gate()
         load_token_scales(xs_win, x_scales)
         load_weight_scales("w1")
-        nc.sync.dma_start(dy_win[:], dy_words[0].rearrange("p t d -> p (t d)").bitcast(I32))
         load_token_scales(dys_win, dy_scales)
-        load_weight_scales("w2t")
-        load_gate()
-        for n in ("w3", "w1t", "w3t"):
+        for n in ("w2t", "w3", "w1t", "w3t"):
             load_weight_scales(n)
-        for n in ("w1t", "w3t"):
-            load_words(nc.sync, n, 0, 2)
-        for n in ("w1", "w2t", "w3", "w1t", "w3t"):
-            load_words(nc.sync, n, 2, 4)
 
         xg = keep.tile([P, T], U32, name="xg", align_bytes=64)
         dyg = keep.tile([P, T], U32, name="dyg", align_bytes=64)
@@ -118,7 +116,7 @@ def tile_moe_rec_glu_sigmoid_kernel(
             gather_x(lo, hi)
             gather_dy(lo, hi)
 
-        dx_sb = keep.tile([P, 4, T], F32, name="dx_sb")
+        dx_sb = [keep.tile([P, 4, C], F32, name="dx_sb%d" % e) for e in range(E)]
         out_sb = [keep.tile([P, T], F32, name="out_sb%d" % kt) for kt in range(4)]
         state = {}
 
@@ -134,8 +132,8 @@ def tile_moe_rec_glu_sigmoid_kernel(
         def as_planes(ap):
             return ap.rearrange("p (t m) -> p t m", t=4)
 
-        def first_product(e, tag, codes, code_scales, n, bufs):
-            bank = psum.tile([P, H], F32, name=tag, bufs=bufs)
+        def first_product(e, place, codes, code_scales, n):
+            bank = psum.tile([P, H], F32, name="first%d" % ((3 * e + place) % 5))
             cols = slice(e * C, (e + 1) * C)
             nc.tensor.matmul_mx(
                 out=bank[:], lhsT=codes[:, cols].bitcast(FP8X4), lhsT_scale=code_scales[:, cols],
@@ -144,9 +142,9 @@ def tile_moe_rec_glu_sigmoid_kernel(
             return bank
 
         def stage_a(e):
-            a1 = first_product(e, "a1", xg, xsg, "w1", 1)
-            dh = first_product(e, "dh", dyg, dysg, "w2t", 2)
-            a3 = first_product(e, "a3", xg, xsg, "w3", 2)
+            a1 = first_product(e, 0, xg, xsg, "w1")
+            dh = first_product(e, 1, dyg, dysg, "w2t")
+            a3 = first_product(e, 2, xg, xsg, "w3")
             s = work.tile([P, H], F32, name="s")
             sn = work.tile([P, H], F32, name="sn")
             nc.scalar.activation(as_planes(s[:]), planes(a1[:]), SIGMOID)
@@ -190,29 +188,26 @@ def tile_moe_rec_glu_sigmoid_kernel(
                         rhs_scale=code_scales[:, j * C : (j + 1) * C],
                         start=(j == 0), stop=(j == 1),
                     )
-            nc.scalar.copy(dx_sb[:, :, e * C : (e + 1) * C], dx[:])
+            nc.scalar.copy(dx_sb[e][:], dx[:])
 
-        def scatter(kt, lo, hi):
-            nc.vector.tensor_copy(out_sb[kt][:].indirect(offsets[:, lo // 16 : hi // 16]), dx_sb[:, kt, lo:hi])
+        def scatter(kt, e):
+            nc.vector.tensor_copy(out_sb[kt][:].indirect(offsets[:, e * C // 16 : (e + 1) * C // 16]), dx_sb[e][:, kt, :])
 
         gather(0, 256)
         gather(256, 512)
         stage_a(0)
         stage_a(1)
         stage_b(0)
-        stage_a(2)
         stage_b(1)
+        stage_a(2)
         stage_c(0)
         stage_a(3)
         stage_b(2)
         stage_c(1)
-        for kt in range(4):
-            scatter(kt, 0, 128)
         stage_b(3)
         stage_c(2)
-        for kt in range(4):
-            scatter(kt, 128, 256)
         stage_c(3)
         for kt in range(4):
-            scatter(kt, 256, 512)
+            for e in range(E):
+                scatter(kt, e)
             nc.sync.dma_start(out[kt * P : (kt + 1) * P, :], out_sb[kt][:])

@@ -52,7 +52,9 @@ def tile_moe_rec_glu_sigmoid_kernel(
         def zero_plane(n):
             zero(ws[n][:].rearrange("p e c -> p (e c)"))
 
+        g_rows = keep.tile([P, C], F32, name="g_rows")
         zero(xs_win[:])
+        nc.vector.memset(g_rows[:], 0.0)
         zero_plane("w1")
         nc.vector.memset(warm_in[:], 0.0)
         nc.scalar.activation(warm_out[:], warm_in[:], SIGMOID)
@@ -77,25 +79,34 @@ def tile_moe_rec_glu_sigmoid_kernel(
             )
 
         def load_gate():
-            with nc.allow_non_contiguous_dma(reason="one gate value a partition and expert"):
-                nc.sync.dma_start(g_col[:], gate[0, :].rearrange("(e u) -> u e", e=E))
+            nc.sync.dma_start(g_rows[0:E, :], gate[0, :].rearrange("(e u) -> e u", e=E))
 
         for n in ("w1t", "w3t"):
             zero_plane(n)
-        for n in ("w1", "w2t", "w3", "w1t"):
-            load_words(nc.gpsimd, n, 0, 4)
+        for n in ("w1", "w2t", "w3"):
+            load_words(nc.gpsimd, n, 0, 2)
         make_identity(nc, ident[:])
-        load_words(nc.gpsimd, "w3t", 0, 4)
 
         nc.sync.dma_start(offsets[:], offs)
         nc.sync.dma_start(x_win[:], x_words[0].rearrange("p t d -> p (t d)").bitcast(I32))
+        load_token_scales(xs_win, x_scales)
         nc.sync.dma_start(dy_win[:], dy_words[0].rearrange("p t d -> p (t d)").bitcast(I32))
         load_gate()
-        load_token_scales(xs_win, x_scales)
         load_weight_scales("w1")
         load_token_scales(dys_win, dy_scales)
-        for n in ("w2t", "w3", "w1t", "w3t"):
+        for n in ("w2t", "w3"):
             load_weight_scales(n)
+        for n in ("w1", "w2t", "w3"):
+            load_words(nc.sync, n, 2, 4)
+        for n in ("w1t", "w3t"):
+            load_weight_scales(n)
+        for lo in (0, 2):
+            for n in ("w1t", "w3t"):
+                load_words(nc.sync, n, lo, lo + 2)
+
+        g_turned = psum.tile([P, 2, C], F32, name="tr1")
+        nc.tensor.transpose(g_turned[:, 0, :], g_rows[:], ident[:])
+        nc.scalar.copy(g_col[:], g_turned[:, 0, 0:E])
 
         xg = keep.tile([P, T], U32, name="xg", align_bytes=64)
         dyg = keep.tile([P, T], U32, name="dyg", align_bytes=64)
@@ -158,7 +169,7 @@ def tile_moe_rec_glu_sigmoid_kernel(
         def stage_b(e):
             da3, u = state[e]
             da1 = work.tile([P, H], BF16, name="da1")
-            nc.vector.tensor_tensor(
+            (nc.vector if e == 0 else nc.gpsimd).tensor_tensor(
                 as_order(da1[:]), da3[:].rearrange("p (u v m) -> p u m v", u=2, v=2), as_order(u[:]), MULT
             )
             tr3 = psum.tile([P, 4, C], F32, name="tr3")

@@ -15,7 +15,9 @@ U8 = mybir.dt.uint8
 FP8X4 = mybir.dt.float8_e4m3fn_x4
 FP4X4 = mybir.dt.float4_e2m1fn_x4
 MULT = mybir.AluOpType.mult
+SUBTRACT = mybir.AluOpType.subtract
 SIGMOID = mybir.ActivationFunctionType.Sigmoid
+SQUARE = mybir.ActivationFunctionType.Square
 COPY = mybir.ActivationFunctionType.Copy
 
 P = 128
@@ -42,6 +44,8 @@ def tile_moe_rec_glu_sigmoid_kernel(
         w = {n: keep.tile([P, E, 1024], U8, name=n + "_w", align_bytes=64) for n in names}
         ws = {n: keep.tile([P, E, 512], U8, name=n + "_s", align_bytes=64) for n in names}
         g_col = keep.tile([P, E], F32, name="g_col")
+        g_neg = keep.tile([P, E], F32, name="g_neg")
+        g_rows = keep.tile([P, C], F32, name="g_rows")
         ident = keep.tile([P, P], F32, name="ident")
         warm_in = keep.tile([P, 1], F32, name="warm_in")
         warm_out = keep.tile([P, 1], F32, name="warm_out")
@@ -52,14 +56,15 @@ def tile_moe_rec_glu_sigmoid_kernel(
         def zero_plane(n):
             zero(ws[n][:].rearrange("p e c -> p (e c)"))
 
-        g_rows = keep.tile([P, C], F32, name="g_rows")
         zero(xs_win[:])
-        nc.vector.memset(g_rows[:], 0.0)
-        zero_plane("w1")
         nc.vector.memset(warm_in[:], 0.0)
         nc.scalar.activation(warm_out[:], warm_in[:], SIGMOID)
+        zero_plane("w1")
         zero(dys_win[:])
-        for n in ("w2t", "w3"):
+        for n in ("w3", "w2t"):
+            zero_plane(n)
+        nc.vector.memset(g_rows[:], 0.0)
+        for n in ("w1t", "w3t"):
             zero_plane(n)
 
         def load_token_scales(tile, src):
@@ -78,70 +83,43 @@ def tile_moe_rec_glu_sigmoid_kernel(
                 w[n][:, lo:hi, :].bitcast(I32), words_in[n][lo:hi, 0, :, :].rearrange("e p c -> p e c").bitcast(I32)
             )
 
-        def load_gate():
-            nc.sync.dma_start(g_rows[0:E, :], gate[0, :].rearrange("(e u) -> e u", e=E))
-
-        for n in ("w1t", "w3t"):
-            zero_plane(n)
-        for n in ("w1", "w2t", "w3"):
+        for n in ("w1", "w3", "w2t"):
             load_words(nc.gpsimd, n, 0, 2)
         make_identity(nc, ident[:])
+        for n in ("w1t", "w3t"):
+            load_words(nc.gpsimd, n, 0, 4)
 
         nc.sync.dma_start(offsets[:], offs)
         nc.sync.dma_start(x_win[:], x_words[0].rearrange("p t d -> p (t d)").bitcast(I32))
-        load_token_scales(xs_win, x_scales)
         nc.sync.dma_start(dy_win[:], dy_words[0].rearrange("p t d -> p (t d)").bitcast(I32))
-        load_gate()
+        load_token_scales(xs_win, x_scales)
         load_weight_scales("w1")
         load_token_scales(dys_win, dy_scales)
-        for n in ("w2t", "w3"):
+        for n in ("w3", "w2t"):
             load_weight_scales(n)
-        for n in ("w1", "w2t", "w3"):
+        nc.sync.dma_start(g_rows[0:E, :], gate[0, :].rearrange("(e u) -> e u", e=E))
+        for n in ("w1", "w3", "w2t"):
             load_words(nc.sync, n, 2, 4)
         for n in ("w1t", "w3t"):
             load_weight_scales(n)
-        for lo in (0, 2):
-            for n in ("w1t", "w3t"):
-                load_words(nc.sync, n, lo, lo + 2)
 
-        g_turned = psum.tile([P, 2, C], F32, name="tr1")
+        g_turned = psum.tile([P, 4, C], F32, name="dx1")
         nc.tensor.transpose(g_turned[:, 0, :], g_rows[:], ident[:])
         nc.scalar.copy(g_col[:], g_turned[:, 0, 0:E])
+        nc.scalar.activation(g_neg[:], g_turned[:, 0, 0:E], COPY, scale=-1.0)
 
         xg = keep.tile([P, T], U32, name="xg", align_bytes=64)
         dyg = keep.tile([P, T], U32, name="dyg", align_bytes=64)
         xsg = keep.tile([P, T], U8, name="xsg", align_bytes=64)
         dysg = keep.tile([P, T], U8, name="dysg", align_bytes=64)
 
-        def gather_x(lo, hi):
-            part = offsets[:, lo // 16 : hi // 16]
-            nc.vector.tensor_copy(xg[:, lo:hi], x_win[:].bitcast(U32).indirect(part))
-            nc.vector.tensor_copy(xsg[:, lo:hi], xs_win[:].indirect(part))
-
-        def gather_dy(lo, hi):
-            part = offsets[:, lo // 16 : hi // 16]
-            nc.vector.tensor_copy(dyg[:, lo:hi], dy_win[:].bitcast(U32).indirect(part))
-            nc.vector.tensor_copy(dysg[:, lo:hi], dys_win[:].indirect(part))
-
-        def gather(lo, hi):
-            gather_x(lo, hi)
-            gather_dy(lo, hi)
+        def gather(into, window, half):
+            lo, hi = half * T // 2, (half + 1) * T // 2
+            nc.vector.tensor_copy(into[:, lo:hi], window.indirect(offsets[:, lo // 16 : hi // 16]))
 
         dx_sb = [keep.tile([P, 4, C], F32, name="dx_sb%d" % e) for e in range(E)]
         out_sb = [keep.tile([P, T], F32, name="out_sb%d" % kt) for kt in range(4)]
         state = {}
-
-        def order(ap):
-            return ap.rearrange("p (m u v) -> p u m v", u=2, v=2)
-
-        def as_order(ap):
-            return ap.rearrange("p (u m v) -> p u m v", u=2, v=2)
-
-        def planes(ap):
-            return ap.rearrange("p (m t) -> p t m", t=4)
-
-        def as_planes(ap):
-            return ap.rearrange("p (t m) -> p t m", t=4)
 
         def first_product(e, place, codes, code_scales, n):
             bank = psum.tile([P, H], F32, name="first%d" % ((3 * e + place) % 5))
@@ -154,33 +132,31 @@ def tile_moe_rec_glu_sigmoid_kernel(
 
         def stage_a(e):
             a1 = first_product(e, 0, xg, xsg, "w1")
-            dh = first_product(e, 1, dyg, dysg, "w2t")
-            a3 = first_product(e, 2, xg, xsg, "w3")
+            a3 = first_product(e, 1, xg, xsg, "w3")
+            dh = first_product(e, 2, dyg, dysg, "w2t")
             s = work.tile([P, H], F32, name="s")
-            sn = work.tile([P, H], F32, name="sn")
-            nc.scalar.activation(as_planes(s[:]), planes(a1[:]), SIGMOID)
-            nc.scalar.activation(as_order(sn[:]), order(a1[:]), SIGMOID, scale=-1.0)
-            da3 = work.tile([P, H], F32, name="da3")
-            nc.vector.scalar_tensor_tensor(as_planes(da3[:]), planes(dh[:]), g_col[:, e : e + 1], as_planes(s[:]), MULT, MULT)
-            u = work.tile([P, H], F32, name="u")
-            nc.vector.tensor_tensor(as_order(u[:]), order(a3[:]), as_order(sn[:]), MULT)
-            state[e] = (da3, u)
+            sq = work.tile([P, H], F32, name="sq")
+            nc.scalar.activation(s[:], a1[:], SIGMOID)
+            nc.scalar.activation(sq[:], s[:], SQUARE, bias=-0.5)
+            da3 = work.tile([P, H], BF16, name="da3")
+            nc.vector.scalar_tensor_tensor(da3[:], dh[:], g_col[:, e : e + 1], s[:], MULT, MULT)
+            v = work.tile([P, H], F32, name="v")
+            nc.vector.scalar_tensor_tensor(v[:], sq[:], 0.25, a3[:], SUBTRACT, MULT)
+            da1 = work.tile([P, H], BF16, name="da1")
+            nc.vector.scalar_tensor_tensor(da1[:], dh[:], g_neg[:, e : e + 1], v[:], MULT, MULT)
+            state[e] = (da1, da3)
 
         def stage_b(e):
-            da3, u = state[e]
-            da1 = work.tile([P, H], BF16, name="da1")
-            (nc.vector if e == 0 else nc.gpsimd).tensor_tensor(
-                as_order(da1[:]), da3[:].rearrange("p (u v m) -> p u m v", u=2, v=2), as_order(u[:]), MULT
-            )
-            tr3 = psum.tile([P, 4, C], F32, name="tr3")
-            tr1 = psum.tile([P, 2, C], F32, name="tr1")
-            for t in range(4):
-                nc.tensor.transpose(tr3[:, t, :], da3[:, t * P : (t + 1) * P], ident[:])
-            for h in range(2):
-                nc.tensor.transpose(tr1[:, h, :], da1[:].bitcast(F32)[:, h * P : (h + 1) * P], ident[:])
+            turned = psum.tile([P, 2, 2, C], F32, name="turned")
+            for j in (1, 0):
+                pairs = state[e][j][:].bitcast(F32)
+                for h in range(2):
+                    nc.tensor.transpose(turned[:, j, h, :], pairs[:, h : 2 * P : 2], ident[:])
             q_in = work.tile([P, 2, C * 4], BF16, name="q_in", align_bytes=64)
-            nc.scalar.activation(q_in[:, 1, :].rearrange("p (c t) -> p c t", t=4), tr3[:].rearrange("p t c -> p c t"), COPY)
-            nc.scalar.copy(q_in[:, 0, :].bitcast(F32).rearrange("p (c h) -> p c h", h=2), tr1[:].rearrange("p h c -> p c h"))
+            nc.scalar.copy(
+                q_in[:].rearrange("p j c -> p (j c)").bitcast(F32).rearrange("p (j c h) -> p j c h", j=2, h=2),
+                turned[:].rearrange("p j h c -> p j c h"),
+            )
             state[e] = q_in
 
         def stage_c(e):
@@ -188,7 +164,7 @@ def tile_moe_rec_glu_sigmoid_kernel(
             codes = work.tile([P, 2 * C], U32, name="codes", align_bytes=64)
             code_scales = work.tile([P, 2 * C], U8, name="code_scales", align_bytes=64)
             nc.vector.quantize_mx(out=codes[:].bitcast(FP8X4), scales=code_scales[:], in_=q_in[:].rearrange("p a c -> p (a c)"))
-            dx = psum.tile([P, 4, C], F32, name="dx")
+            dx = psum.tile([P, 4, C], F32, name="dx%d" % (e % 2))
             for kt in range(4):
                 for j, n in enumerate(("w1t", "w3t")):
                     nc.tensor.matmul_mx(
@@ -201,24 +177,24 @@ def tile_moe_rec_glu_sigmoid_kernel(
                     )
             nc.scalar.copy(dx_sb[e][:], dx[:])
 
-        def scatter(kt, e):
-            nc.vector.tensor_copy(out_sb[kt][:].indirect(offsets[:, e * C // 16 : (e + 1) * C // 16]), dx_sb[e][:, kt, :])
+        def scatter(e):
+            for kt in range(4):
+                nc.vector.tensor_copy(out_sb[kt][:].indirect(offsets[:, e * C // 16 : (e + 1) * C // 16]), dx_sb[e][:, kt, :])
+                if e == E - 1:
+                    nc.sync.dma_start(out[kt * P : (kt + 1) * P, :], out_sb[kt][:])
 
-        gather(0, 256)
-        gather(256, 512)
+        for half in range(2):
+            gather(xg, x_win[:].bitcast(U32), half)
+        for half in range(2):
+            gather(dyg, dy_win[:].bitcast(U32), half)
+        for half in range(2):
+            gather(xsg, xs_win[:], half)
+            gather(dysg, dys_win[:], half)
         stage_a(0)
-        stage_a(1)
-        stage_b(0)
-        stage_b(1)
-        stage_a(2)
-        stage_c(0)
-        stage_a(3)
-        stage_b(2)
-        stage_c(1)
-        stage_b(3)
-        stage_c(2)
-        stage_c(3)
-        for kt in range(4):
-            for e in range(E):
-                scatter(kt, e)
-            nc.sync.dma_start(out[kt * P : (kt + 1) * P, :], out_sb[kt][:])
+        for e in range(E):
+            stage_b(e)
+            stage_c(e)
+            if e + 1 < E:
+                stage_a(e + 1)
+        for e in range(E):
+            scatter(e)

@@ -63,9 +63,6 @@ def tile_moe_rec_glu_sigmoid_kernel(
         zero(dys_win[:])
         for n in ("w3", "w2t"):
             zero_plane(n)
-        nc.vector.memset(g_rows[:], 0.0)
-        for n in ("w1t", "w3t"):
-            zero_plane(n)
 
         def load_token_scales(tile, src):
             for r in range(4):
@@ -83,14 +80,18 @@ def tile_moe_rec_glu_sigmoid_kernel(
                 w[n][:, lo:hi, :].bitcast(I32), words_in[n][lo:hi, 0, :, :].rearrange("e p c -> p e c").bitcast(I32)
             )
 
-        for n in ("w1", "w3", "w2t"):
+        for n in ("w3", "w2t"):
             load_words(nc.gpsimd, n, 0, 2)
+        nc.gpsimd.memset(g_rows[:], 0.0)
         make_identity(nc, ident[:])
         for n in ("w1t", "w3t"):
-            load_words(nc.gpsimd, n, 0, 4)
+            nc.gpsimd.memset(ws[n][:].rearrange("p e c -> p (e c)").bitcast(I32), 0)
+        for n in ("w1t", "w3t"):
+            load_words(nc.gpsimd, n, 0, 2)
 
         nc.sync.dma_start(offsets[:], offs)
         nc.sync.dma_start(x_win[:], x_words[0].rearrange("p t d -> p (t d)").bitcast(I32))
+        load_words(nc.sync, "w1", 0, 2)
         nc.sync.dma_start(dy_win[:], dy_words[0].rearrange("p t d -> p (t d)").bitcast(I32))
         load_token_scales(xs_win, x_scales)
         load_weight_scales("w1")
@@ -102,6 +103,8 @@ def tile_moe_rec_glu_sigmoid_kernel(
             load_words(nc.sync, n, 2, 4)
         for n in ("w1t", "w3t"):
             load_weight_scales(n)
+        for n in ("w1t", "w3t"):
+            load_words(nc.sync, n, 2, E)
 
         g_turned = psum.tile([P, 4, C], F32, name="dx1")
         nc.tensor.transpose(g_turned[:, 0, :], g_rows[:], ident[:])
@@ -117,7 +120,7 @@ def tile_moe_rec_glu_sigmoid_kernel(
             lo, hi = half * T // 2, (half + 1) * T // 2
             nc.vector.tensor_copy(into[:, lo:hi], window.indirect(offsets[:, lo // 16 : hi // 16]))
 
-        dx_sb = [keep.tile([P, 4, C], F32, name="dx_sb%d" % e) for e in range(E)]
+        dx_sb = {}
         out_sb = [keep.tile([P, T], F32, name="out_sb%d" % kt) for kt in range(4)]
         state = {}
 
@@ -138,16 +141,26 @@ def tile_moe_rec_glu_sigmoid_kernel(
             sq = work.tile([P, H], F32, name="sq")
             nc.scalar.activation(s[:], a1[:], SIGMOID)
             nc.scalar.activation(sq[:], s[:], SQUARE, bias=-0.5)
-            da3 = work.tile([P, H], BF16, name="da3")
-            nc.vector.scalar_tensor_tensor(da3[:], dh[:], g_col[:, e : e + 1], s[:], MULT, MULT)
+            if e > 0:
+                state["d", e] = work.tile([P, H], F32, name="d")
+                nc.scalar.activation(state["d", e][:], dh[:], COPY, scale=g_neg[:, e : e + 1])
+            state[e] = (a3, dh, s, sq)
+
+        def products(e):
+            a3, dh, s, sq = state[e]
             v = work.tile([P, H], F32, name="v")
             nc.vector.scalar_tensor_tensor(v[:], sq[:], 0.25, a3[:], SUBTRACT, MULT)
+            da3 = work.tile([P, H], BF16, name="da3")
+            nc.vector.scalar_tensor_tensor(da3[:], dh[:], g_col[:, e : e + 1], s[:], MULT, MULT)
             da1 = work.tile([P, H], BF16, name="da1")
-            nc.vector.scalar_tensor_tensor(da1[:], dh[:], g_neg[:, e : e + 1], v[:], MULT, MULT)
+            if e == 0:
+                nc.vector.scalar_tensor_tensor(da1[:], dh[:], g_neg[:, e : e + 1], v[:], MULT, MULT)
+            else:
+                nc.gpsimd.tensor_tensor(da1[:], state["d", e][:], v[:], MULT)
             state[e] = (da1, da3)
 
         def stage_b(e):
-            turned = psum.tile([P, 2, 2, C], F32, name="turned")
+            turned = psum.tile([P, 2, 2, C], F32, name="turned" if e < 2 else "dx0")
             for j in (1, 0):
                 pairs = state[e][j][:].bitcast(F32)
                 for h in range(2):
@@ -161,21 +174,28 @@ def tile_moe_rec_glu_sigmoid_kernel(
 
         def stage_c(e):
             q_in = state[e]
-            codes = work.tile([P, 2 * C], U32, name="codes", align_bytes=64)
+            codes = keep.tile([P, 2 * C], U32, name="codes%d" % e if e < 2 else "dx_sb%d" % (e - 2), align_bytes=64)
             code_scales = work.tile([P, 2 * C], U8, name="code_scales", align_bytes=64)
             nc.vector.quantize_mx(out=codes[:].bitcast(FP8X4), scales=code_scales[:], in_=q_in[:].rearrange("p a c -> p (a c)"))
-            dx = psum.tile([P, 4, C], F32, name="dx%d" % (e % 2))
-            for kt in range(4):
-                for j, n in enumerate(("w1t", "w3t")):
-                    nc.tensor.matmul_mx(
-                        out=dx[:, kt, :],
-                        lhsT=w[n][:, e, 2 * P * kt : 2 * P * (kt + 1)].bitcast(FP4X4),
-                        lhsT_scale=ws[n][:, e, P * kt : P * (kt + 1)],
-                        rhs=codes[:, j * C : (j + 1) * C].bitcast(FP8X4),
-                        rhs_scale=code_scales[:, j * C : (j + 1) * C],
-                        start=(j == 0), stop=(j == 1),
-                    )
-            nc.scalar.copy(dx_sb[e][:], dx[:])
+            state[e] = (codes, code_scales)
+
+        def second_products(e):
+            codes, code_scales = state[e]
+            dx_sb[e] = keep.tile([P, 4, C], F32, name="dx_sb%d" % e, align_bytes=64)
+            parts = ((0, 1, "dx0"), (1, 4, "dx1")) if e == 0 else ((0, 4, "dx%d" % (e % 2)),)
+            for lo, hi, bank in parts:
+                dx = psum.tile([P, 4, C], F32, name=bank)
+                for kt in range(lo, hi):
+                    for j, n in enumerate(("w1t", "w3t")):
+                        nc.tensor.matmul_mx(
+                            out=dx[:, kt, :],
+                            lhsT=w[n][:, e, 2 * P * kt : 2 * P * (kt + 1)].bitcast(FP4X4),
+                            lhsT_scale=ws[n][:, e, P * kt : P * (kt + 1)],
+                            rhs=codes[:, j * C : (j + 1) * C].bitcast(FP8X4),
+                            rhs_scale=code_scales[:, j * C : (j + 1) * C],
+                            start=(j == 0), stop=(j == 1),
+                        )
+                nc.scalar.copy(dx_sb[e][:, lo:hi, :], dx[:, lo:hi, :])
 
         def scatter(e):
             for kt in range(4):
@@ -190,11 +210,21 @@ def tile_moe_rec_glu_sigmoid_kernel(
         for half in range(2):
             gather(xsg, xs_win[:], half)
             gather(dysg, dys_win[:], half)
-        stage_a(0)
-        for e in range(E):
+        for e in range(2):
+            stage_a(e)
+            products(e)
+        for e in range(2):
             stage_b(e)
+            stage_a(e + 2)
             stage_c(e)
-            if e + 1 < E:
-                stage_a(e + 1)
-        for e in range(E):
+            products(e + 2)
+        for e in range(2):
+            second_products(e)
+        for e in range(2, E):
+            stage_b(e)
+        for e in range(2):
+            scatter(e)
+            stage_c(e + 2)
+            second_products(e + 2)
+        for e in range(2, E):
             scatter(e)

@@ -21,6 +21,9 @@ SQUARE = mybir.ActivationFunctionType.Square
 COPY = mybir.ActivationFunctionType.Copy
 
 P = 128
+BLOCKS = K // P
+EARLY = E // 2
+FIRST_BANKS = 5
 
 
 def tile_moe_rec_glu_sigmoid_kernel(
@@ -30,7 +33,7 @@ def tile_moe_rec_glu_sigmoid_kernel(
     nc = tc.nc
     with ExitStack() as ctx:
         keep = ctx.enter_context(tc.tile_pool(name="keep", bufs=1))
-        work = ctx.enter_context(tc.tile_pool(name="work", bufs=4))
+        work = ctx.enter_context(tc.tile_pool(name="work", bufs=E))
         psum = ctx.enter_context(tc.psum_pool(name="psum", bufs=1))
 
         offsets = keep.tile([P, T // 16], U16, name="offsets")
@@ -47,8 +50,6 @@ def tile_moe_rec_glu_sigmoid_kernel(
         g_neg = keep.tile([P, E], F32, name="g_neg")
         g_rows = keep.tile([P, C], F32, name="g_rows")
         ident = keep.tile([P, P], F32, name="ident")
-        warm_in = keep.tile([P, 1], F32, name="warm_in")
-        warm_out = keep.tile([P, 1], F32, name="warm_out")
 
         def zero(tile):
             nc.vector.memset(tile.bitcast(I32), 0)
@@ -57,8 +58,6 @@ def tile_moe_rec_glu_sigmoid_kernel(
             zero(ws[n][:].rearrange("p e c -> p (e c)"))
 
         zero(xs_win[:])
-        nc.vector.memset(warm_in[:], 0.0)
-        nc.scalar.activation(warm_out[:], warm_in[:], SIGMOID)
         zero_plane("w1")
         zero(dys_win[:])
         for n in ("w3", "w2t"):
@@ -81,17 +80,17 @@ def tile_moe_rec_glu_sigmoid_kernel(
             )
 
         for n in ("w3", "w2t"):
-            load_words(nc.gpsimd, n, 0, 2)
+            load_words(nc.gpsimd, n, 0, EARLY)
         nc.gpsimd.memset(g_rows[:], 0.0)
         make_identity(nc, ident[:])
         for n in ("w1t", "w3t"):
             nc.gpsimd.memset(ws[n][:].rearrange("p e c -> p (e c)").bitcast(I32), 0)
         for n in ("w1t", "w3t"):
-            load_words(nc.gpsimd, n, 0, 2)
+            load_words(nc.gpsimd, n, 0, EARLY)
 
         nc.sync.dma_start(offsets[:], offs)
         nc.sync.dma_start(x_win[:], x_words[0].rearrange("p t d -> p (t d)").bitcast(I32))
-        load_words(nc.sync, "w1", 0, 2)
+        load_words(nc.sync, "w1", 0, EARLY)
         nc.sync.dma_start(dy_win[:], dy_words[0].rearrange("p t d -> p (t d)").bitcast(I32))
         load_token_scales(xs_win, x_scales)
         load_weight_scales("w1")
@@ -100,13 +99,13 @@ def tile_moe_rec_glu_sigmoid_kernel(
             load_weight_scales(n)
         nc.sync.dma_start(g_rows[0:E, :], gate[0, :].rearrange("(e u) -> e u", e=E))
         for n in ("w1", "w3", "w2t"):
-            load_words(nc.sync, n, 2, 4)
+            load_words(nc.sync, n, EARLY, E)
         for n in ("w1t", "w3t"):
             load_weight_scales(n)
         for n in ("w1t", "w3t"):
-            load_words(nc.sync, n, 2, E)
+            load_words(nc.sync, n, EARLY, E)
 
-        g_turned = psum.tile([P, 4, C], F32, name="dx1")
+        g_turned = psum.tile([P, BLOCKS, C], F32, name="dx1")
         nc.tensor.transpose(g_turned[:, 0, :], g_rows[:], ident[:])
         nc.scalar.copy(g_col[:], g_turned[:, 0, 0:E])
         nc.scalar.activation(g_neg[:], g_turned[:, 0, 0:E], COPY, scale=-1.0)
@@ -120,12 +119,11 @@ def tile_moe_rec_glu_sigmoid_kernel(
             lo, hi = half * T // 2, (half + 1) * T // 2
             nc.vector.tensor_copy(into[:, lo:hi], window.indirect(offsets[:, lo // 16 : hi // 16]))
 
-        dx_sb = {}
-        out_sb = [keep.tile([P, T], F32, name="out_sb%d" % kt) for kt in range(4)]
-        state = {}
+        out_sb = [keep.tile([P, T], F32, name="out_sb%d" % kt) for kt in range(BLOCKS)]
+        firsts, minus_dh, gradients, q_ins, quantised, dx_sb = {}, {}, {}, {}, {}, {}
 
         def first_product(e, place, codes, code_scales, n):
-            bank = psum.tile([P, H], F32, name="first%d" % ((3 * e + place) % 5))
+            bank = psum.tile([P, H], F32, name="first%d" % ((3 * e + place) % FIRST_BANKS))
             cols = slice(e * C, (e + 1) * C)
             nc.tensor.matmul_mx(
                 out=bank[:], lhsT=codes[:, cols].bitcast(FP8X4), lhsT_scale=code_scales[:, cols],
@@ -133,58 +131,59 @@ def tile_moe_rec_glu_sigmoid_kernel(
             )
             return bank
 
-        def stage_a(e):
+        def first_stage(e):
             a1 = first_product(e, 0, xg, xsg, "w1")
             a3 = first_product(e, 1, xg, xsg, "w3")
-            dh = first_product(e, 2, dyg, dysg, "w2t")
+            raw_dh = first_product(e, 2, dyg, dysg, "w2t")
             s = work.tile([P, H], F32, name="s")
             sq = work.tile([P, H], F32, name="sq")
             nc.scalar.activation(s[:], a1[:], SIGMOID)
             nc.scalar.activation(sq[:], s[:], SQUARE, bias=-0.5)
             if e > 0:
-                state["d", e] = work.tile([P, H], F32, name="d")
-                nc.scalar.activation(state["d", e][:], dh[:], COPY, scale=g_neg[:, e : e + 1])
-            state[e] = (a3, dh, s, sq)
+                minus_dh[e] = work.tile([P, H], F32, name="d")
+                nc.scalar.activation(minus_dh[e][:], raw_dh[:], COPY, scale=g_neg[:, e : e + 1])
+            firsts[e] = (a3, raw_dh, s, sq)
 
         def products(e):
-            a3, dh, s, sq = state[e]
+            a3, raw_dh, s, sq = firsts[e]
             v = work.tile([P, H], F32, name="v")
             nc.vector.scalar_tensor_tensor(v[:], sq[:], 0.25, a3[:], SUBTRACT, MULT)
             da3 = work.tile([P, H], BF16, name="da3")
-            nc.vector.scalar_tensor_tensor(da3[:], dh[:], g_col[:, e : e + 1], s[:], MULT, MULT)
+            nc.vector.scalar_tensor_tensor(da3[:], raw_dh[:], g_col[:, e : e + 1], s[:], MULT, MULT)
             da1 = work.tile([P, H], BF16, name="da1")
             if e == 0:
-                nc.vector.scalar_tensor_tensor(da1[:], dh[:], g_neg[:, e : e + 1], v[:], MULT, MULT)
+                nc.vector.scalar_tensor_tensor(da1[:], raw_dh[:], g_neg[:, e : e + 1], v[:], MULT, MULT)
             else:
-                nc.gpsimd.tensor_tensor(da1[:], state["d", e][:], v[:], MULT)
-            state[e] = (da1, da3)
+                nc.gpsimd.tensor_tensor(da1[:], minus_dh[e][:], v[:], MULT)
+            gradients[e] = (da1, da3)
 
-        def stage_b(e):
-            turned = psum.tile([P, 2, 2, C], F32, name="turned" if e < 2 else "dx0")
+        def turn(e):
+            turned = psum.tile([P, 2, 2, C], F32, name="turned" if e < EARLY else "dx0")
             for j in (1, 0):
-                pairs = state[e][j][:].bitcast(F32)
+                pairs = gradients[e][j][:].bitcast(F32)
                 for h in range(2):
                     nc.tensor.transpose(turned[:, j, h, :], pairs[:, h : 2 * P : 2], ident[:])
-            q_in = work.tile([P, 2, C * 4], BF16, name="q_in", align_bytes=64)
+            q_ins[e] = work.tile([P, 2, C * 4], BF16, name="q_in", align_bytes=64)
             nc.scalar.copy(
-                q_in[:].rearrange("p j c -> p (j c)").bitcast(F32).rearrange("p (j c h) -> p j c h", j=2, h=2),
+                q_ins[e][:].rearrange("p j c -> p (j c)").bitcast(F32).rearrange("p (j c h) -> p j c h", j=2, h=2),
                 turned[:].rearrange("p j h c -> p j c h"),
             )
-            state[e] = q_in
 
-        def stage_c(e):
-            q_in = state[e]
-            codes = keep.tile([P, 2 * C], U32, name="codes%d" % e if e < 2 else "dx_sb%d" % (e - 2), align_bytes=64)
+        def quantise(e):
+            buffer_name = "codes%d" % e if e < EARLY else "dx_sb%d" % (e - EARLY)
+            codes = keep.tile([P, 2 * C], U32, name=buffer_name, align_bytes=64)
             code_scales = work.tile([P, 2 * C], U8, name="code_scales", align_bytes=64)
-            nc.vector.quantize_mx(out=codes[:].bitcast(FP8X4), scales=code_scales[:], in_=q_in[:].rearrange("p a c -> p (a c)"))
-            state[e] = (codes, code_scales)
+            nc.vector.quantize_mx(
+                out=codes[:].bitcast(FP8X4), scales=code_scales[:], in_=q_ins[e][:].rearrange("p j c -> p (j c)")
+            )
+            quantised[e] = (codes, code_scales)
 
         def second_products(e):
-            codes, code_scales = state[e]
-            dx_sb[e] = keep.tile([P, 4, C], F32, name="dx_sb%d" % e, align_bytes=64)
-            parts = ((0, 1, "dx0"), (1, 4, "dx1")) if e == 0 else ((0, 4, "dx%d" % (e % 2)),)
-            for lo, hi, bank in parts:
-                dx = psum.tile([P, 4, C], F32, name=bank)
+            codes, code_scales = quantised[e]
+            dx_sb[e] = keep.tile([P, BLOCKS, C], F32, name="dx_sb%d" % e, align_bytes=64)
+            parts = ((0, 1, "dx0"), (1, BLOCKS, "dx1")) if e == 0 else ((0, BLOCKS, "dx%d" % (e % 2)),)
+            for lo, hi, bank_name in parts:
+                dx = psum.tile([P, BLOCKS, C], F32, name=bank_name)
                 for kt in range(lo, hi):
                     for j, n in enumerate(("w1t", "w3t")):
                         nc.tensor.matmul_mx(
@@ -198,8 +197,10 @@ def tile_moe_rec_glu_sigmoid_kernel(
                 nc.scalar.copy(dx_sb[e][:, lo:hi, :], dx[:, lo:hi, :])
 
         def scatter(e):
-            for kt in range(4):
-                nc.vector.tensor_copy(out_sb[kt][:].indirect(offsets[:, e * C // 16 : (e + 1) * C // 16]), dx_sb[e][:, kt, :])
+            for kt in range(BLOCKS):
+                nc.vector.tensor_copy(
+                    out_sb[kt][:].indirect(offsets[:, e * C // 16 : (e + 1) * C // 16]), dx_sb[e][:, kt, :]
+                )
                 if e == E - 1:
                     nc.sync.dma_start(out[kt * P : (kt + 1) * P, :], out_sb[kt][:])
 
@@ -210,21 +211,21 @@ def tile_moe_rec_glu_sigmoid_kernel(
         for half in range(2):
             gather(xsg, xs_win[:], half)
             gather(dysg, dys_win[:], half)
-        for e in range(2):
-            stage_a(e)
+        for e in range(EARLY):
+            first_stage(e)
             products(e)
-        for e in range(2):
-            stage_b(e)
-            stage_a(e + 2)
-            stage_c(e)
-            products(e + 2)
-        for e in range(2):
+        for e in range(EARLY):
+            turn(e)
+            first_stage(e + EARLY)
+            quantise(e)
+            products(e + EARLY)
+        for e in range(EARLY):
             second_products(e)
-        for e in range(2, E):
-            stage_b(e)
-        for e in range(2):
+        for e in range(EARLY, E):
+            turn(e)
+        for e in range(EARLY):
             scatter(e)
-            stage_c(e + 2)
-            second_products(e + 2)
-        for e in range(2, E):
+            quantise(e + EARLY)
+            second_products(e + EARLY)
+        for e in range(EARLY, E):
             scatter(e)

@@ -198,9 +198,11 @@ def tile_moe_rec_glu_sigmoid_kernel(
 
         def scatter(e):
             for kt in range(BLOCKS):
-                nc.vector.tensor_copy(
-                    out_sb[kt][:].indirect(offsets[:, e * C // 16 : (e + 1) * C // 16]), dx_sb[e][:, kt, :]
-                )
+                window = out_sb[kt][:].indirect(offsets[:, e * C // 16 : (e + 1) * C // 16])
+                if kt % 2 == 0:
+                    nc.vector.tensor_copy(window, dx_sb[e][:, kt, :])
+                else:
+                    nc.scalar.activation(window, dx_sb[e][:, kt, :], COPY)
                 if e == E - 1:
                     nc.sync.dma_start(out[kt * P : (kt + 1) * P, :], out_sb[kt][:])
 

@@ -16,6 +16,7 @@ FP8X4 = mybir.dt.float8_e4m3fn_x4
 FP4X4 = mybir.dt.float4_e2m1fn_x4
 MULT = mybir.AluOpType.mult
 SUBTRACT = mybir.AluOpType.subtract
+ADD = mybir.AluOpType.add
 SIGMOID = mybir.ActivationFunctionType.Sigmoid
 SQUARE = mybir.ActivationFunctionType.Square
 COPY = mybir.ActivationFunctionType.Copy
@@ -23,6 +24,7 @@ COPY = mybir.ActivationFunctionType.Copy
 P = 128
 BLOCKS = K // P
 EARLY = E // 2
+STAGE = 4
 FIRST_BANKS = 5
 
 
@@ -40,75 +42,65 @@ def tile_moe_rec_glu_sigmoid_kernel(
         x_win = keep.tile([P, T], I32, name="x_win", align_bytes=64)
         dy_win = keep.tile([P, T], I32, name="dy_win", align_bytes=64)
         xs_win = keep.tile([P, T], U8, name="xs_win", align_bytes=64)
-        dys_win = keep.tile([P, T], U8, name="dys_win", align_bytes=64)
-        names = ("w1", "w2t", "w3", "w1t", "w3t")
+        first_names, second_names = ("w1", "w3", "w2t"), ("w1t", "w3t")
         words_in = {"w1": w1_words, "w2t": w2t_words, "w3": w3_words, "w1t": w1t_words, "w3t": w3t_words}
         scales_in = {"w1": w1_scales, "w2t": w2t_scales, "w3": w3_scales, "w1t": w1t_scales, "w3t": w3t_scales}
-        w = {n: keep.tile([P, E, 1024], U8, name=n + "_w", align_bytes=64) for n in names}
-        ws = {n: keep.tile([P, E, 512], U8, name=n + "_s", align_bytes=64) for n in names}
+        first_planes = keep.tile([P, 3, E, 512], U8, name="first_planes", align_bytes=64)
+        second_planes = keep.tile([P, 2, E, 512], U8, name="second_planes", align_bytes=64)
+        ws = {n: first_planes[:, m, :, :] for m, n in enumerate(first_names)}
+        for m, n in enumerate(second_names):
+            ws[n] = second_planes[:, m, :, :]
         g_col = keep.tile([P, E], F32, name="g_col")
         g_neg = keep.tile([P, E], F32, name="g_neg")
-        g_rows = keep.tile([P, C], F32, name="g_rows")
         ident = keep.tile([P, P], F32, name="ident")
+        w = {}
 
         def zero(tile):
             nc.vector.memset(tile.bitcast(I32), 0)
-
-        def zero_plane(n):
-            zero(ws[n][:].rearrange("p e c -> p (e c)"))
-
-        zero(xs_win[:])
-        zero_plane("w1")
-        zero(dys_win[:])
-        for n in ("w3", "w2t"):
-            zero_plane(n)
 
         def load_token_scales(tile, src):
             for r in range(4):
                 nc.sync.dma_start(tile[r:P:32, :].bitcast(I32), src[0, r:16:4, :].bitcast(I32))
 
-        def load_weight_scales(n):
+        def load_words(queue, n, lo, into):
+            queue.dma_start(
+                into.bitcast(I32), words_in[n][lo : lo + EARLY, 0, :, :].rearrange("e p c -> p e c").bitcast(I32)
+            )
+            for e in range(EARLY):
+                w[n, lo + e] = into[:, e, :]
+
+        def stage_scales(names, buffer_name):
+            staged = keep.tile([P, len(names), E, 512], U8, name=buffer_name, align_bytes=64)
+            for m, n in enumerate(names):
+                nc.sync.dma_start(
+                    staged[STAGE : STAGE + 16, m, :, :].bitcast(I32),
+                    scales_in[n][:, 0, :, :].rearrange("e b c -> b e c").bitcast(I32),
+                )
+            return staged
+
+        def spread_scales(staged, planes):
             for r in range(4):
                 nc.sync.dma_start(
-                    ws[n][r:P:32, :, :].bitcast(I32),
-                    scales_in[n][:, 0, r:16:4, :].rearrange("e b c -> b e c").bitcast(I32),
+                    planes[r:P:32, :, :, :].rearrange("p m e c -> p (m e c)").bitcast(I32),
+                    staged[STAGE + r : STAGE + 16 : 4, :, :, :].rearrange("p m e c -> p (m e c)").bitcast(I32),
                 )
 
-        def load_words(queue, n, lo, hi):
-            queue.dma_start(
-                w[n][:, lo:hi, :].bitcast(I32), words_in[n][lo:hi, 0, :, :].rearrange("e p c -> p e c").bitcast(I32)
-            )
-
-        for n in ("w3", "w2t"):
-            load_words(nc.gpsimd, n, 0, EARLY)
-        nc.gpsimd.memset(g_rows[:], 0.0)
+        early = {n: keep.tile([P, EARLY, 1024], U8, name=n + "_early", align_bytes=64) for n in words_in}
+        zero(xs_win[:])
+        zero(first_planes[:].rearrange("p m e c -> p (m e c)"))
+        for n in first_names:
+            load_words(nc.gpsimd, n, 0, early[n][:])
         make_identity(nc, ident[:])
-        for n in ("w1t", "w3t"):
-            nc.gpsimd.memset(ws[n][:].rearrange("p e c -> p (e c)").bitcast(I32), 0)
-        for n in ("w1t", "w3t"):
-            load_words(nc.gpsimd, n, 0, EARLY)
+        nc.gpsimd.memset(second_planes[:].rearrange("p m e c -> p (m e c)").bitcast(I32), 0)
+        for n in second_names:
+            load_words(nc.gpsimd, n, 0, early[n][:])
 
         nc.sync.dma_start(offsets[:], offs)
         nc.sync.dma_start(x_win[:], x_words[0].rearrange("p t d -> p (t d)").bitcast(I32))
-        load_words(nc.sync, "w1", 0, EARLY)
         nc.sync.dma_start(dy_win[:], dy_words[0].rearrange("p t d -> p (t d)").bitcast(I32))
+        staged = stage_scales(first_names, "staged")
         load_token_scales(xs_win, x_scales)
-        load_weight_scales("w1")
-        load_token_scales(dys_win, dy_scales)
-        for n in ("w3", "w2t"):
-            load_weight_scales(n)
-        nc.sync.dma_start(g_rows[0:E, :], gate[0, :].rearrange("(e u) -> e u", e=E))
-        for n in ("w1", "w3", "w2t"):
-            load_words(nc.sync, n, EARLY, E)
-        for n in ("w1t", "w3t"):
-            load_weight_scales(n)
-        for n in ("w1t", "w3t"):
-            load_words(nc.sync, n, EARLY, E)
-
-        g_turned = psum.tile([P, BLOCKS, C], F32, name="dx1")
-        nc.tensor.transpose(g_turned[:, 0, :], g_rows[:], ident[:])
-        nc.scalar.copy(g_col[:], g_turned[:, 0, 0:E])
-        nc.scalar.activation(g_neg[:], g_turned[:, 0, 0:E], COPY, scale=-1.0)
+        spread_scales(staged, first_planes)
 
         xg = keep.tile([P, T], U32, name="xg", align_bytes=64)
         dyg = keep.tile([P, T], U32, name="dyg", align_bytes=64)
@@ -119,15 +111,50 @@ def tile_moe_rec_glu_sigmoid_kernel(
             lo, hi = half * T // 2, (half + 1) * T // 2
             nc.vector.tensor_copy(into[:, lo:hi], window.indirect(offsets[:, lo // 16 : hi // 16]))
 
-        out_sb = [keep.tile([P, T], F32, name="out_sb%d" % kt) for kt in range(BLOCKS)]
-        firsts, minus_dh, gradients, q_ins, quantised, dx_sb = {}, {}, {}, {}, {}, {}
+        for half in range(2):
+            gather(xg, x_win[:].bitcast(U32), half)
+        dys_win = keep.tile([P, T], U8, name="x_win", align_bytes=64)
+        zero(dys_win[:])
+        load_token_scales(dys_win, dy_scales)
+        for half in range(2):
+            gather(dyg, dy_win[:].bitcast(U32), half)
+        g_rows = keep.tile([P, C], F32, name="dy_win", align_bytes=64)
+        nc.sync.dma_start(g_rows[:], gate.rearrange("r (e u) -> (r e) u", e=E)[0:P, :])
+        for half in range(2):
+            gather(xsg, xs_win[:], half)
+        late = keep.tile([P, 3, EARLY, 1024], U8, name="staged", align_bytes=64)
+        for m, n in enumerate(first_names):
+            load_words(nc.sync, n, EARLY, late[:, m, :, :])
+        for n in second_names:
+            for r in range(4):
+                nc.sync.dma_start(
+                    ws[n][r:P:32, :, :].bitcast(I32),
+                    scales_in[n][:, 0, r:16:4, :].rearrange("e b c -> b e c").bitcast(I32),
+                )
+        for half in range(2):
+            gather(dysg, dys_win[:], half)
+
+        def turn_gate():
+            g_turned = psum.tile([P, H], F32, name="first0")
+            nc.tensor.transpose(g_turned[:, 0:P], g_rows[:], ident[:])
+            nc.scalar.copy(g_col[:], g_turned[:, 0:E])
+            nc.scalar.activation(g_neg[:], g_turned[:, 0:E], COPY, scale=-1.0)
+
+        out_sb, firsts, gradients, q_ins, quantised, dx_sb = {}, {}, {}, {}, {}, {}
+
+        first_banks = (
+            ("first0", "first1", "first2"),
+            ("first3", "first4", "dx0"),
+            ("dx0", "first1", "first0"),
+            ("first3", "first4", "first2"),
+        )
 
         def first_product(e, place, codes, code_scales, n):
-            bank = psum.tile([P, H], F32, name="first%d" % ((3 * e + place) % FIRST_BANKS))
+            bank = psum.tile([P, H], F32, name=first_banks[e][place])
             cols = slice(e * C, (e + 1) * C)
             nc.tensor.matmul_mx(
                 out=bank[:], lhsT=codes[:, cols].bitcast(FP8X4), lhsT_scale=code_scales[:, cols],
-                rhs=w[n][:, e, :].bitcast(FP4X4), rhs_scale=ws[n][:, e, :], start=True, stop=True,
+                rhs=w[n, e].bitcast(FP4X4), rhs_scale=ws[n][:, e, :], start=True, stop=True,
             )
             return bank
 
@@ -135,99 +162,115 @@ def tile_moe_rec_glu_sigmoid_kernel(
             a1 = first_product(e, 0, xg, xsg, "w1")
             a3 = first_product(e, 1, xg, xsg, "w3")
             raw_dh = first_product(e, 2, dyg, dysg, "w2t")
-            s = work.tile([P, H], F32, name="s")
-            sq = work.tile([P, H], F32, name="sq")
+            s = keep.tile([P, H], F32, name="s%d" % e, align_bytes=64)
             nc.scalar.activation(s[:], a1[:], SIGMOID)
-            nc.scalar.activation(sq[:], s[:], SQUARE, bias=-0.5)
-            if e > 0:
-                minus_dh[e] = work.tile([P, H], F32, name="d")
-                nc.scalar.activation(minus_dh[e][:], raw_dh[:], COPY, scale=g_neg[:, e : e + 1])
-            firsts[e] = (a3, raw_dh, s, sq)
+            firsts[e] = (a3, raw_dh, s)
 
         def products(e):
-            a3, raw_dh, s, sq = firsts[e]
-            v = work.tile([P, H], F32, name="v")
-            nc.vector.scalar_tensor_tensor(v[:], sq[:], 0.25, a3[:], SUBTRACT, MULT)
-            da3 = work.tile([P, H], BF16, name="da3")
-            nc.vector.scalar_tensor_tensor(da3[:], raw_dh[:], g_col[:, e : e + 1], s[:], MULT, MULT)
-            da1 = work.tile([P, H], BF16, name="da1")
+            a3, raw_dh, s = firsts[e]
+            grad = keep.tile([P, 2, H], BF16, name="grad%d" % e, align_bytes=64)
             if e == 0:
-                nc.vector.scalar_tensor_tensor(da1[:], raw_dh[:], g_neg[:, e : e + 1], v[:], MULT, MULT)
+                sq = work.tile([P, H], F32, name="sq")
+                nc.scalar.activation(sq[:], s[:], SQUARE, bias=-0.5)
+                turn_gate()
+                v = work.tile([P, H], F32, name="v")
+                nc.vector.scalar_tensor_tensor(v[:], sq[:], 0.25, a3[:], SUBTRACT, MULT)
+                nc.vector.scalar_tensor_tensor(grad[:, 1, :], raw_dh[:], g_col[:, e : e + 1], s[:], MULT, MULT)
+                nc.vector.scalar_tensor_tensor(grad[:, 0, :], raw_dh[:], g_neg[:, e : e + 1], v[:], MULT, MULT)
             else:
-                nc.gpsimd.tensor_tensor(da1[:], minus_dh[e][:], v[:], MULT)
-            gradients[e] = (da1, da3)
+                minus_da3 = work.tile([P, H], F32, name="minus_da3")
+                u = work.tile([P, H], F32, name="u")
+                if e == 1:
+                    minus_dh = work.tile([P, H], F32, name="minus_dh")
+                    nc.scalar.activation(minus_dh[:], raw_dh[:], COPY, scale=g_neg[:, e : e + 1])
+                    nc.gpsimd.tensor_tensor(minus_da3[:], minus_dh[:], s[:], MULT)
+                else:
+                    nc.vector.scalar_tensor_tensor(minus_da3[:], raw_dh[:], g_neg[:, e : e + 1], s[:], MULT, MULT)
+                nc.vector.scalar_tensor_tensor(u[:], s[:], 1.0, a3[:], SUBTRACT, MULT)
+                if e < E - 1:
+                    nc.scalar.activation(grad[:, 1, :], minus_da3[:], COPY, scale=-1.0)
+                else:
+                    nc.gpsimd.tensor_scalar(grad[:, 1, :], minus_da3[:], -1.0, 0.0, MULT, ADD)
+                nc.gpsimd.tensor_tensor(grad[:, 0, :], minus_da3[:], u[:], MULT)
+            gradients[e] = grad
 
         def turn(e):
-            turned = psum.tile([P, 2, 2, C], F32, name="turned" if e < EARLY else "dx0")
+            turned = psum.tile([P, 2, 2, C], F32, name="turned")
             for j in (1, 0):
-                pairs = gradients[e][j][:].bitcast(F32)
+                pairs = gradients[e][:, j, :].bitcast(F32)
                 for h in range(2):
                     nc.tensor.transpose(turned[:, j, h, :], pairs[:, h : 2 * P : 2], ident[:])
-            q_ins[e] = work.tile([P, 2, C * 4], BF16, name="q_in", align_bytes=64)
+            q_ins[e] = keep.tile([P, 2, C * 4], BF16, name="q_in%d" % e, align_bytes=64)
             nc.scalar.copy(
                 q_ins[e][:].rearrange("p j c -> p (j c)").bitcast(F32).rearrange("p (j c h) -> p j c h", j=2, h=2),
                 turned[:].rearrange("p j h c -> p j c h"),
             )
 
         def quantise(e):
-            buffer_name = "codes%d" % e if e < EARLY else "dx_sb%d" % (e - EARLY)
-            codes = keep.tile([P, 2 * C], U32, name=buffer_name, align_bytes=64)
+            codes = work.tile([P, 2 * C], U32, name="codes", align_bytes=64)
             code_scales = work.tile([P, 2 * C], U8, name="code_scales", align_bytes=64)
             nc.vector.quantize_mx(
                 out=codes[:].bitcast(FP8X4), scales=code_scales[:], in_=q_ins[e][:].rearrange("p j c -> p (j c)")
             )
             quantised[e] = (codes, code_scales)
 
+        dx_parts = (
+            ((0, 1, "dx0", nc.scalar.copy), (1, 4, "dx1", nc.scalar.copy)),
+            ((0, 4, "dx0", nc.scalar.copy),),
+            ((0, 2, "dx1", nc.scalar.copy), (2, 4, "first3", nc.vector.tensor_copy)),
+            ((0, 2, "dx0", nc.scalar.copy), (2, 4, "first4", nc.vector.tensor_copy)),
+        )
+
         def second_products(e):
             codes, code_scales = quantised[e]
-            dx_sb[e] = keep.tile([P, BLOCKS, C], F32, name="dx_sb%d" % e, align_bytes=64)
-            parts = ((0, 1, "dx0"), (1, BLOCKS, "dx1")) if e == 0 else ((0, BLOCKS, "dx%d" % (e % 2)),)
-            for lo, hi, bank_name in parts:
+            buffer_name = "dx_sb%d" % e
+            dx_sb[e] = keep.tile([P, BLOCKS, C], F32, name=buffer_name, align_bytes=64)
+            for lo, hi, bank_name, copy in dx_parts[e]:
                 dx = psum.tile([P, BLOCKS, C], F32, name=bank_name)
                 for kt in range(lo, hi):
                     for j, n in enumerate(("w1t", "w3t")):
                         nc.tensor.matmul_mx(
                             out=dx[:, kt, :],
-                            lhsT=w[n][:, e, 2 * P * kt : 2 * P * (kt + 1)].bitcast(FP4X4),
+                            lhsT=w[n, e][:, 2 * P * kt : 2 * P * (kt + 1)].bitcast(FP4X4),
                             lhsT_scale=ws[n][:, e, P * kt : P * (kt + 1)],
                             rhs=codes[:, j * C : (j + 1) * C].bitcast(FP8X4),
                             rhs_scale=code_scales[:, j * C : (j + 1) * C],
                             start=(j == 0), stop=(j == 1),
                         )
-                nc.scalar.copy(dx_sb[e][:, lo:hi, :], dx[:, lo:hi, :])
+                copy(dx_sb[e][:, lo:hi, :], dx[:, lo:hi, :])
+
+        out_buffers = ("out0", "grad3", "s3", "q_in2")
 
         def scatter(e):
             for kt in range(BLOCKS):
+                if e == 0:
+                    out_sb[kt] = keep.tile([P, T], F32, name=out_buffers[kt], align_bytes=64)
                 window = out_sb[kt][:].indirect(offsets[:, e * C // 16 : (e + 1) * C // 16])
-                if kt % 2 == 0:
-                    nc.vector.tensor_copy(window, dx_sb[e][:, kt, :])
-                else:
+                if kt < 2:
                     nc.scalar.activation(window, dx_sb[e][:, kt, :], COPY)
+                else:
+                    nc.vector.tensor_copy(window, dx_sb[e][:, kt, :])
                 if e == E - 1:
                     nc.sync.dma_start(out[kt * P : (kt + 1) * P, :], out_sb[kt][:])
 
-        for half in range(2):
-            gather(xg, x_win[:].bitcast(U32), half)
-        for half in range(2):
-            gather(dyg, dy_win[:].bitcast(U32), half)
-        for half in range(2):
-            gather(xsg, xs_win[:], half)
-            gather(dysg, dys_win[:], half)
         for e in range(EARLY):
             first_stage(e)
             products(e)
-        for e in range(EARLY):
-            turn(e)
-            first_stage(e + EARLY)
+        last = keep.tile([P, 2, EARLY, 1024], U8, name="w2t_early", align_bytes=64)
+        for m, n in enumerate(second_names):
+            load_words(nc.sync, n, EARLY, last[:, m, :, :])
+        first_stage(2)
+        turn(0)
+        products(2)
+        first_stage(3)
+        quantise(0)
+        turn(1)
+        products(3)
+        for e in range(1, E):
+            second_products(e - 1)
             quantise(e)
-            products(e + EARLY)
-        for e in range(EARLY):
-            second_products(e)
-        for e in range(EARLY, E):
-            turn(e)
-        for e in range(EARLY):
-            scatter(e)
-            quantise(e + EARLY)
-            second_products(e + EARLY)
-        for e in range(EARLY, E):
+            if e + 1 < E:
+                turn(e + 1)
+        second_products(E - 1)
+        for e in range(E):
             scatter(e)

@@ -16,7 +16,6 @@ FP8X4 = mybir.dt.float8_e4m3fn_x4
 FP4X4 = mybir.dt.float4_e2m1fn_x4
 MULT = mybir.AluOpType.mult
 SUBTRACT = mybir.AluOpType.subtract
-ADD = mybir.AluOpType.add
 SIGMOID = mybir.ActivationFunctionType.Sigmoid
 SQUARE = mybir.ActivationFunctionType.Square
 COPY = mybir.ActivationFunctionType.Copy
@@ -24,7 +23,6 @@ COPY = mybir.ActivationFunctionType.Copy
 P = 128
 BLOCKS = K // P
 EARLY = E // 2
-STAGE = 4
 FIRST_BANKS = 5
 
 
@@ -42,65 +40,75 @@ def tile_moe_rec_glu_sigmoid_kernel(
         x_win = keep.tile([P, T], I32, name="x_win", align_bytes=64)
         dy_win = keep.tile([P, T], I32, name="dy_win", align_bytes=64)
         xs_win = keep.tile([P, T], U8, name="xs_win", align_bytes=64)
-        first_names, second_names = ("w1", "w3", "w2t"), ("w1t", "w3t")
+        dys_win = keep.tile([P, T], U8, name="dys_win", align_bytes=64)
+        names = ("w1", "w2t", "w3", "w1t", "w3t")
         words_in = {"w1": w1_words, "w2t": w2t_words, "w3": w3_words, "w1t": w1t_words, "w3t": w3t_words}
         scales_in = {"w1": w1_scales, "w2t": w2t_scales, "w3": w3_scales, "w1t": w1t_scales, "w3t": w3t_scales}
-        first_planes = keep.tile([P, 3, E, 512], U8, name="first_planes", align_bytes=64)
-        second_planes = keep.tile([P, 2, E, 512], U8, name="second_planes", align_bytes=64)
-        ws = {n: first_planes[:, m, :, :] for m, n in enumerate(first_names)}
-        for m, n in enumerate(second_names):
-            ws[n] = second_planes[:, m, :, :]
+        w = {n: keep.tile([P, E, 1024], U8, name=n + "_w", align_bytes=64) for n in names}
+        ws = {n: keep.tile([P, E, 512], U8, name=n + "_s", align_bytes=64) for n in names}
         g_col = keep.tile([P, E], F32, name="g_col")
         g_neg = keep.tile([P, E], F32, name="g_neg")
+        g_rows = keep.tile([P, C], F32, name="g_rows")
         ident = keep.tile([P, P], F32, name="ident")
-        w = {}
 
         def zero(tile):
             nc.vector.memset(tile.bitcast(I32), 0)
+
+        def zero_plane(n):
+            zero(ws[n][:].rearrange("p e c -> p (e c)"))
+
+        zero(xs_win[:])
+        zero_plane("w1")
+        zero(dys_win[:])
+        for n in ("w3", "w2t"):
+            zero_plane(n)
 
         def load_token_scales(tile, src):
             for r in range(4):
                 nc.sync.dma_start(tile[r:P:32, :].bitcast(I32), src[0, r:16:4, :].bitcast(I32))
 
-        def load_words(queue, n, lo, into):
-            queue.dma_start(
-                into.bitcast(I32), words_in[n][lo : lo + EARLY, 0, :, :].rearrange("e p c -> p e c").bitcast(I32)
-            )
-            for e in range(EARLY):
-                w[n, lo + e] = into[:, e, :]
-
-        def stage_scales(names, buffer_name):
-            staged = keep.tile([P, len(names), E, 512], U8, name=buffer_name, align_bytes=64)
-            for m, n in enumerate(names):
-                nc.sync.dma_start(
-                    staged[STAGE : STAGE + 16, m, :, :].bitcast(I32),
-                    scales_in[n][:, 0, :, :].rearrange("e b c -> b e c").bitcast(I32),
-                )
-            return staged
-
-        def spread_scales(staged, planes):
+        def load_weight_scales(n):
             for r in range(4):
                 nc.sync.dma_start(
-                    planes[r:P:32, :, :, :].rearrange("p m e c -> p (m e c)").bitcast(I32),
-                    staged[STAGE + r : STAGE + 16 : 4, :, :, :].rearrange("p m e c -> p (m e c)").bitcast(I32),
+                    ws[n][r:P:32, :, :].bitcast(I32),
+                    scales_in[n][:, 0, r:16:4, :].rearrange("e b c -> b e c").bitcast(I32),
                 )
 
-        early = {n: keep.tile([P, EARLY, 1024], U8, name=n + "_early", align_bytes=64) for n in words_in}
-        zero(xs_win[:])
-        zero(first_planes[:].rearrange("p m e c -> p (m e c)"))
-        for n in first_names:
-            load_words(nc.gpsimd, n, 0, early[n][:])
+        def load_words(queue, n, lo, hi):
+            queue.dma_start(
+                w[n][:, lo:hi, :].bitcast(I32), words_in[n][lo:hi, 0, :, :].rearrange("e p c -> p e c").bitcast(I32)
+            )
+
+        for n in ("w3", "w2t"):
+            load_words(nc.gpsimd, n, 0, EARLY)
+        nc.gpsimd.memset(g_rows[:], 0.0)
         make_identity(nc, ident[:])
-        nc.gpsimd.memset(second_planes[:].rearrange("p m e c -> p (m e c)").bitcast(I32), 0)
-        for n in second_names:
-            load_words(nc.gpsimd, n, 0, early[n][:])
+        for n in ("w1t", "w3t"):
+            nc.gpsimd.memset(ws[n][:].rearrange("p e c -> p (e c)").bitcast(I32), 0)
+        for n in ("w1t", "w3t"):
+            load_words(nc.gpsimd, n, 0, EARLY)
 
         nc.sync.dma_start(offsets[:], offs)
         nc.sync.dma_start(x_win[:], x_words[0].rearrange("p t d -> p (t d)").bitcast(I32))
+        load_words(nc.sync, "w1", 0, EARLY)
         nc.sync.dma_start(dy_win[:], dy_words[0].rearrange("p t d -> p (t d)").bitcast(I32))
-        staged = stage_scales(first_names, "staged")
         load_token_scales(xs_win, x_scales)
-        spread_scales(staged, first_planes)
+        load_weight_scales("w1")
+        load_token_scales(dys_win, dy_scales)
+        for n in ("w3", "w2t"):
+            load_weight_scales(n)
+        nc.sync.dma_start(g_rows[0:E, :], gate[0, :].rearrange("(e u) -> e u", e=E))
+        for n in ("w1", "w3", "w2t"):
+            load_words(nc.sync, n, EARLY, E)
+        for n in ("w1t", "w3t"):
+            load_weight_scales(n)
+        for n in ("w1t", "w3t"):
+            load_words(nc.sync, n, EARLY, E)
+
+        g_turned = psum.tile([P, BLOCKS, C], F32, name="dx1")
+        nc.tensor.transpose(g_turned[:, 0, :], g_rows[:], ident[:])
+        nc.scalar.copy(g_col[:], g_turned[:, 0, 0:E])
+        nc.scalar.activation(g_neg[:], g_turned[:, 0, 0:E], COPY, scale=-1.0)
 
         xg = keep.tile([P, T], U32, name="xg", align_bytes=64)
         dyg = keep.tile([P, T], U32, name="dyg", align_bytes=64)
@@ -113,40 +121,20 @@ def tile_moe_rec_glu_sigmoid_kernel(
 
         for half in range(2):
             gather(xg, x_win[:].bitcast(U32), half)
-        dys_win = keep.tile([P, T], U8, name="x_win", align_bytes=64)
-        zero(dys_win[:])
-        load_token_scales(dys_win, dy_scales)
         for half in range(2):
             gather(dyg, dy_win[:].bitcast(U32), half)
-        g_rows = keep.tile([P, C], F32, name="dy_win", align_bytes=64)
-        nc.sync.dma_start(g_rows[:], gate.rearrange("r (e u) -> (r e) u", e=E)[0:P, :])
         for half in range(2):
             gather(xsg, xs_win[:], half)
-        late = keep.tile([P, 3, EARLY, 1024], U8, name="staged", align_bytes=64)
-        for m, n in enumerate(first_names):
-            load_words(nc.sync, n, EARLY, late[:, m, :, :])
-        for n in second_names:
-            for r in range(4):
-                nc.sync.dma_start(
-                    ws[n][r:P:32, :, :].bitcast(I32),
-                    scales_in[n][:, 0, r:16:4, :].rearrange("e b c -> b e c").bitcast(I32),
-                )
-        for half in range(2):
             gather(dysg, dys_win[:], half)
 
-        def turn_gate():
-            g_turned = psum.tile([P, H], F32, name="first0")
-            nc.tensor.transpose(g_turned[:, 0:P], g_rows[:], ident[:])
-            nc.scalar.copy(g_col[:], g_turned[:, 0:E])
-            nc.scalar.activation(g_neg[:], g_turned[:, 0:E], COPY, scale=-1.0)
-
+        slopes = {}
         out_sb, firsts, gradients, q_ins, quantised, dx_sb = {}, {}, {}, {}, {}, {}
 
         first_banks = (
             ("first0", "first1", "first2"),
             ("first3", "first4", "dx0"),
-            ("dx0", "first1", "first0"),
-            ("first3", "first4", "first2"),
+            ("first0", "first1", "first2"),
+            ("first3", "first4", "first0"),
         )
 
         def first_product(e, place, codes, code_scales, n):
@@ -154,7 +142,7 @@ def tile_moe_rec_glu_sigmoid_kernel(
             cols = slice(e * C, (e + 1) * C)
             nc.tensor.matmul_mx(
                 out=bank[:], lhsT=codes[:, cols].bitcast(FP8X4), lhsT_scale=code_scales[:, cols],
-                rhs=w[n, e].bitcast(FP4X4), rhs_scale=ws[n][:, e, :], start=True, stop=True,
+                rhs=w[n][:, e, :].bitcast(FP4X4), rhs_scale=ws[n][:, e, :], start=True, stop=True,
             )
             return bank
 
@@ -166,41 +154,27 @@ def tile_moe_rec_glu_sigmoid_kernel(
             nc.scalar.activation(s[:], a1[:], SIGMOID)
             firsts[e] = (a3, raw_dh, s)
 
+        def slope(e):
+            a3, raw_dh, s = firsts[e]
+            sq = work.tile([P, H], F32, name="sq")
+            nc.scalar.activation(sq[:], s[:], SQUARE, bias=-0.5)
+            slopes[e] = work.tile([P, H], F32, name="v")
+            nc.vector.scalar_tensor_tensor(slopes[e][:], sq[:], 0.25, a3[:], SUBTRACT, MULT)
+
         def products(e):
             a3, raw_dh, s = firsts[e]
-            grad = keep.tile([P, 2, H], BF16, name="grad%d" % e, align_bytes=64)
-            if e == 0:
-                sq = work.tile([P, H], F32, name="sq")
-                nc.scalar.activation(sq[:], s[:], SQUARE, bias=-0.5)
-                turn_gate()
-                v = work.tile([P, H], F32, name="v")
-                nc.vector.scalar_tensor_tensor(v[:], sq[:], 0.25, a3[:], SUBTRACT, MULT)
-                nc.vector.scalar_tensor_tensor(grad[:, 1, :], raw_dh[:], g_col[:, e : e + 1], s[:], MULT, MULT)
-                nc.vector.scalar_tensor_tensor(grad[:, 0, :], raw_dh[:], g_neg[:, e : e + 1], v[:], MULT, MULT)
-            else:
-                minus_da3 = work.tile([P, H], F32, name="minus_da3")
-                u = work.tile([P, H], F32, name="u")
-                if e == 1:
-                    minus_dh = work.tile([P, H], F32, name="minus_dh")
-                    nc.scalar.activation(minus_dh[:], raw_dh[:], COPY, scale=g_neg[:, e : e + 1])
-                    nc.gpsimd.tensor_tensor(minus_da3[:], minus_dh[:], s[:], MULT)
-                else:
-                    nc.vector.scalar_tensor_tensor(minus_da3[:], raw_dh[:], g_neg[:, e : e + 1], s[:], MULT, MULT)
-                nc.vector.scalar_tensor_tensor(u[:], s[:], 1.0, a3[:], SUBTRACT, MULT)
-                if e < E - 1:
-                    nc.scalar.activation(grad[:, 1, :], minus_da3[:], COPY, scale=-1.0)
-                else:
-                    nc.gpsimd.tensor_scalar(grad[:, 1, :], minus_da3[:], -1.0, 0.0, MULT, ADD)
-                nc.gpsimd.tensor_tensor(grad[:, 0, :], minus_da3[:], u[:], MULT)
+            grad = keep.tile([P, 2, H], BF16, name=("grad0", "grad1", "q_in0", "q_in1")[e], align_bytes=64)
+            nc.vector.scalar_tensor_tensor(grad[:, 1, :], s[:], g_col[:, e : e + 1], raw_dh[:], MULT, MULT)
+            nc.vector.scalar_tensor_tensor(grad[:, 0, :], slopes[e][:], g_neg[:, e : e + 1], raw_dh[:], MULT, MULT)
             gradients[e] = grad
 
         def turn(e):
-            turned = psum.tile([P, 2, 2, C], F32, name="turned")
+            turned = psum.tile([P, 2, 2, C], F32, name=("turned", "turned", "dx0", "dx1")[e])
             for j in (1, 0):
                 pairs = gradients[e][:, j, :].bitcast(F32)
                 for h in range(2):
                     nc.tensor.transpose(turned[:, j, h, :], pairs[:, h : 2 * P : 2], ident[:])
-            q_ins[e] = keep.tile([P, 2, C * 4], BF16, name="q_in%d" % e, align_bytes=64)
+            q_ins[e] = keep.tile([P, 2, C * 4], BF16, name=("q_in0", "q_in1", "dx00", "q_in3")[e], align_bytes=64)
             nc.scalar.copy(
                 q_ins[e][:].rearrange("p j c -> p (j c)").bitcast(F32).rearrange("p (j c h) -> p j c h", j=2, h=2),
                 turned[:].rearrange("p j h c -> p j c h"),
@@ -214,63 +188,56 @@ def tile_moe_rec_glu_sigmoid_kernel(
             )
             quantised[e] = (codes, code_scales)
 
-        dx_parts = (
-            ((0, 1, "dx0", nc.scalar.copy), (1, 4, "dx1", nc.scalar.copy)),
-            ((0, 4, "dx0", nc.scalar.copy),),
-            ((0, 2, "dx1", nc.scalar.copy), (2, 4, "first3", nc.vector.tensor_copy)),
-            ((0, 2, "dx0", nc.scalar.copy), (2, 4, "first4", nc.vector.tensor_copy)),
-        )
+        dx_banks = (("dx0", "dx1"), ("turned", "first1"), ("first2", "first3"), ("first4", "first0"))
 
         def second_products(e):
             codes, code_scales = quantised[e]
-            buffer_name = "dx_sb%d" % e
-            dx_sb[e] = keep.tile([P, BLOCKS, C], F32, name=buffer_name, align_bytes=64)
-            for lo, hi, bank_name, copy in dx_parts[e]:
-                dx = psum.tile([P, BLOCKS, C], F32, name=bank_name)
-                for kt in range(lo, hi):
+            for half in ((0, 1) if e == 0 else (1, 0)):
+                copy = nc.vector.tensor_copy if e > 0 and half == 1 else nc.scalar.copy
+                dx = psum.tile([P, 2, C], F32, name=dx_banks[e][half])
+                for b in range(2):
+                    kt = 2 * half + b
                     for j, n in enumerate(("w1t", "w3t")):
                         nc.tensor.matmul_mx(
-                            out=dx[:, kt, :],
-                            lhsT=w[n, e][:, 2 * P * kt : 2 * P * (kt + 1)].bitcast(FP4X4),
+                            out=dx[:, b, :],
+                            lhsT=w[n][:, e, 2 * P * kt : 2 * P * (kt + 1)].bitcast(FP4X4),
                             lhsT_scale=ws[n][:, e, P * kt : P * (kt + 1)],
                             rhs=codes[:, j * C : (j + 1) * C].bitcast(FP8X4),
                             rhs_scale=code_scales[:, j * C : (j + 1) * C],
                             start=(j == 0), stop=(j == 1),
                         )
-                copy(dx_sb[e][:, lo:hi, :], dx[:, lo:hi, :])
-
-        out_buffers = ("out0", "grad3", "s3", "q_in2")
+                dx_sb[e, half] = keep.tile([P, 2, C], F32, name="dx%d%d" % (e, half), align_bytes=64)
+                copy(dx_sb[e, half][:], dx[:])
 
         def scatter(e):
             for kt in range(BLOCKS):
                 if e == 0:
-                    out_sb[kt] = keep.tile([P, T], F32, name=out_buffers[kt], align_bytes=64)
+                    out_sb[kt] = keep.tile([P, T], F32, name="out%d" % kt)
                 window = out_sb[kt][:].indirect(offsets[:, e * C // 16 : (e + 1) * C // 16])
                 if kt < 2:
-                    nc.scalar.activation(window, dx_sb[e][:, kt, :], COPY)
+                    nc.scalar.activation(window, dx_sb[e, 0][:, kt, :], COPY)
                 else:
-                    nc.vector.tensor_copy(window, dx_sb[e][:, kt, :])
+                    nc.vector.tensor_copy(window, dx_sb[e, 1][:, kt - 2, :])
                 if e == E - 1:
                     nc.sync.dma_start(out[kt * P : (kt + 1) * P, :], out_sb[kt][:])
 
         for e in range(EARLY):
             first_stage(e)
+            slope(e)
+        for e in range(EARLY):
             products(e)
-        last = keep.tile([P, 2, EARLY, 1024], U8, name="w2t_early", align_bytes=64)
-        for m, n in enumerate(second_names):
-            load_words(nc.sync, n, EARLY, last[:, m, :, :])
-        first_stage(2)
-        turn(0)
-        products(2)
-        first_stage(3)
-        quantise(0)
-        turn(1)
-        products(3)
-        for e in range(1, E):
-            second_products(e - 1)
+        for e in range(EARLY):
+            first_stage(e + EARLY)
+            turn(e)
+            slope(e + EARLY)
             quantise(e)
-            if e + 1 < E:
-                turn(e + 1)
+            products(e + EARLY)
+        second_products(0)
+        scatter(0)
+        for e in range(EARLY, E):
+            turn(e)
+            quantise(e)
+            second_products(e - 1)
         second_products(E - 1)
-        for e in range(E):
+        for e in range(1, E):
             scatter(e)

@@ -127,18 +127,11 @@ def tile_moe_rec_glu_sigmoid_kernel(
             gather(xsg, xs_win[:], half)
             gather(dysg, dys_win[:], half)
 
-        slopes = {}
+        slopes, squares, minus_dh = {}, {}, {}
         out_sb, firsts, gradients, q_ins, quantised, dx_sb = {}, {}, {}, {}, {}, {}
 
-        first_banks = (
-            ("first0", "first1", "first2"),
-            ("first3", "first4", "dx0"),
-            ("first0", "first1", "first2"),
-            ("first3", "first4", "first0"),
-        )
-
         def first_product(e, place, codes, code_scales, n):
-            bank = psum.tile([P, H], F32, name=first_banks[e][place])
+            bank = psum.tile([P, H], F32, name="first%d" % ((3 * e + place) % FIRST_BANKS))
             cols = slice(e * C, (e + 1) * C)
             nc.tensor.matmul_mx(
                 out=bank[:], lhsT=codes[:, cols].bitcast(FP8X4), lhsT_scale=code_scales[:, cols],
@@ -152,20 +145,27 @@ def tile_moe_rec_glu_sigmoid_kernel(
             raw_dh = first_product(e, 2, dyg, dysg, "w2t")
             s = keep.tile([P, H], F32, name="s%d" % e, align_bytes=64)
             nc.scalar.activation(s[:], a1[:], SIGMOID)
+            squares[e] = work.tile([P, H], F32, name="sq")
+            nc.scalar.activation(squares[e][:], s[:], SQUARE, bias=-0.5)
+            if e > 0:
+                minus_dh[e] = work.tile([P, H], F32, name="minus_dh")
+                nc.scalar.activation(minus_dh[e][:], raw_dh[:], COPY, scale=g_neg[:, e : e + 1])
             firsts[e] = (a3, raw_dh, s)
 
         def slope(e):
             a3, raw_dh, s = firsts[e]
-            sq = work.tile([P, H], F32, name="sq")
-            nc.scalar.activation(sq[:], s[:], SQUARE, bias=-0.5)
+            sq = squares[e]
             slopes[e] = work.tile([P, H], F32, name="v")
             nc.vector.scalar_tensor_tensor(slopes[e][:], sq[:], 0.25, a3[:], SUBTRACT, MULT)
 
         def products(e):
             a3, raw_dh, s = firsts[e]
-            grad = keep.tile([P, 2, H], BF16, name=("grad0", "grad1", "q_in0", "q_in1")[e], align_bytes=64)
+            grad = keep.tile([P, 2, H], BF16, name="grad%d" % e, align_bytes=64)
             nc.vector.scalar_tensor_tensor(grad[:, 1, :], s[:], g_col[:, e : e + 1], raw_dh[:], MULT, MULT)
-            nc.vector.scalar_tensor_tensor(grad[:, 0, :], slopes[e][:], g_neg[:, e : e + 1], raw_dh[:], MULT, MULT)
+            if e == 0:
+                nc.vector.scalar_tensor_tensor(grad[:, 0, :], slopes[e][:], g_neg[:, e : e + 1], raw_dh[:], MULT, MULT)
+            else:
+                nc.gpsimd.tensor_tensor(grad[:, 0, :], minus_dh[e][:], slopes[e][:], MULT)
             gradients[e] = grad
 
         def turn(e):
@@ -188,7 +188,7 @@ def tile_moe_rec_glu_sigmoid_kernel(
             )
             quantised[e] = (codes, code_scales)
 
-        dx_banks = (("dx0", "dx1"), ("turned", "first1"), ("first2", "first3"), ("first4", "first0"))
+        dx_banks = (("dx0", "dx1"), ("turned", "first2"), ("first3", "first4"), ("first0", "first1"))
 
         def second_products(e):
             codes, code_scales = quantised[e]
@@ -219,18 +219,18 @@ def tile_moe_rec_glu_sigmoid_kernel(
                 else:
                     nc.vector.tensor_copy(window, dx_sb[e, 1][:, kt - 2, :])
                 if e == E - 1:
-                    nc.sync.dma_start(out[kt * P : (kt + 1) * P, :], out_sb[kt][:])
+                    queue = nc.scalar if kt == 1 else nc.sync
+                    queue.dma_start(out[kt * P : (kt + 1) * P, :], out_sb[kt][:])
 
         for e in range(EARLY):
             first_stage(e)
             slope(e)
-        for e in range(EARLY):
             products(e)
         for e in range(EARLY):
-            first_stage(e + EARLY)
             turn(e)
-            slope(e + EARLY)
+            first_stage(e + EARLY)
             quantise(e)
+            slope(e + EARLY)
             products(e + EARLY)
         second_products(0)
         scatter(0)

@@ -139,31 +139,43 @@ def tile_moe_rec_glu_sigmoid_kernel(
             )
             return bank
 
+        def paired(bank):
+            return bank[:].rearrange("q (p h b) -> q h p b", h=2, b=2)
+
+        def halves(tile):
+            return tile.rearrange("q (h p b) -> q h p b", h=2, b=2)
+
+        def product(into, left, scalar, bank, op):
+            for h in range(2):
+                nc.vector.scalar_tensor_tensor(
+                    halves(into)[:, h, :, :], halves(left)[:, h, :, :], scalar, paired(bank)[:, h, :, :], op, MULT
+                )
+
         def first_stage(e):
             a1 = first_product(e, 0, xg, xsg, "w1")
             a3 = first_product(e, 1, xg, xsg, "w3")
             raw_dh = first_product(e, 2, dyg, dysg, "w2t")
             s = keep.tile([P, H], F32, name="s%d" % e, align_bytes=64)
-            nc.scalar.activation(s[:], a1[:], SIGMOID)
+            nc.scalar.activation(halves(s[:]), paired(a1), SIGMOID)
             squares[e] = work.tile([P, H], F32, name="sq")
             nc.scalar.activation(squares[e][:], s[:], SQUARE, bias=-0.5)
             if e > 0:
                 minus_dh[e] = work.tile([P, H], F32, name="minus_dh")
-                nc.scalar.activation(minus_dh[e][:], raw_dh[:], COPY, scale=g_neg[:, e : e + 1])
+                nc.scalar.activation(halves(minus_dh[e][:]), paired(raw_dh), COPY, scale=g_neg[:, e : e + 1])
             firsts[e] = (a3, raw_dh, s)
 
         def slope(e):
             a3, raw_dh, s = firsts[e]
             sq = squares[e]
             slopes[e] = work.tile([P, H], F32, name="v")
-            nc.vector.scalar_tensor_tensor(slopes[e][:], sq[:], 0.25, a3[:], SUBTRACT, MULT)
+            product(slopes[e][:], sq[:], 0.25, a3, SUBTRACT)
 
         def products(e):
             a3, raw_dh, s = firsts[e]
             grad = keep.tile([P, 2, H], BF16, name="grad%d" % e, align_bytes=64)
-            nc.vector.scalar_tensor_tensor(grad[:, 1, :], s[:], g_col[:, e : e + 1], raw_dh[:], MULT, MULT)
+            product(grad[:, 1, :], s[:], g_col[:, e : e + 1], raw_dh, MULT)
             if e == 0:
-                nc.vector.scalar_tensor_tensor(grad[:, 0, :], slopes[e][:], g_neg[:, e : e + 1], raw_dh[:], MULT, MULT)
+                product(grad[:, 0, :], slopes[e][:], g_neg[:, e : e + 1], raw_dh, MULT)
             else:
                 nc.gpsimd.tensor_tensor(grad[:, 0, :], minus_dh[e][:], slopes[e][:], MULT)
             gradients[e] = grad
@@ -173,7 +185,7 @@ def tile_moe_rec_glu_sigmoid_kernel(
             for j in (1, 0):
                 pairs = gradients[e][:, j, :].bitcast(F32)
                 for h in range(2):
-                    nc.tensor.transpose(turned[:, j, h, :], pairs[:, h : 2 * P : 2], ident[:])
+                    nc.tensor.transpose(turned[:, j, h, :], pairs[:, h * P : (h + 1) * P], ident[:])
             q_ins[e] = keep.tile([P, 2, C * 4], BF16, name=("q_in0", "q_in1", "dx00", "q_in3")[e], align_bytes=64)
             nc.scalar.copy(
                 q_ins[e][:].rearrange("p j c -> p (j c)").bitcast(F32).rearrange("p (j c h) -> p j c h", j=2, h=2),

@@ -23,6 +23,7 @@ COPY = mybir.ActivationFunctionType.Copy
 P = 128
 BLOCKS = K // P
 EARLY = E // 2
+SCALAR_BLOCKS = BLOCKS // 2
 FIRST_BANKS = 5
 
 
@@ -90,9 +91,9 @@ def tile_moe_rec_glu_sigmoid_kernel(
 
         nc.sync.dma_start(offsets[:], offs)
         nc.sync.dma_start(x_win[:], x_words[0].rearrange("p t d -> p (t d)").bitcast(I32))
-        load_words(nc.sync, "w1", 0, EARLY)
-        nc.sync.dma_start(dy_win[:], dy_words[0].rearrange("p t d -> p (t d)").bitcast(I32))
         load_token_scales(xs_win, x_scales)
+        nc.sync.dma_start(dy_win[:], dy_words[0].rearrange("p t d -> p (t d)").bitcast(I32))
+        load_words(nc.sync, "w1", 0, EARLY)
         load_weight_scales("w1")
         load_token_scales(dys_win, dy_scales)
         for n in ("w3", "w2t"):
@@ -119,16 +120,13 @@ def tile_moe_rec_glu_sigmoid_kernel(
             lo, hi = half * T // 2, (half + 1) * T // 2
             nc.vector.tensor_copy(into[:, lo:hi], window.indirect(offsets[:, lo // 16 : hi // 16]))
 
-        for half in range(2):
-            gather(xg, x_win[:].bitcast(U32), half)
-        for half in range(2):
-            gather(dyg, dy_win[:].bitcast(U32), half)
-        for half in range(2):
-            gather(xsg, xs_win[:], half)
-            gather(dysg, dys_win[:], half)
+        windows = (x_win[:].bitcast(U32), xs_win[:], dy_win[:].bitcast(U32), dys_win[:])
+        for into, window in zip((xg, xsg, dyg, dysg), windows):
+            for half in range(2):
+                gather(into, window, half)
 
-        slopes, squares, minus_dh = {}, {}, {}
-        out_sb, firsts, gradients, q_ins, quantised, dx_sb = {}, {}, {}, {}, {}, {}
+        squares, minus_dh, firsts, gradients = {}, {}, {}, {}
+        q_ins, quantised, dx_psum, dx_sb, out_sb = {}, {}, {}, {}, {}
 
         def first_product(e, place, codes, code_scales, n):
             bank = psum.tile([P, H], F32, name="first%d" % ((3 * e + place) % FIRST_BANKS))
@@ -139,16 +137,17 @@ def tile_moe_rec_glu_sigmoid_kernel(
             )
             return bank
 
-        def paired(bank):
-            return bank[:].rearrange("q (p h b) -> q h p b", h=2, b=2)
+        def bank_in_pairs(bank):
+            return bank[:].rearrange("q (p h d) -> q h p d", h=2, d=2)
 
-        def halves(tile):
-            return tile.rearrange("q (h p b) -> q h p b", h=2, b=2)
+        def tile_in_pairs(values):
+            return values.rearrange("q (h p d) -> q h p d", h=2, d=2)
 
-        def product(into, left, scalar, bank, op):
+        def times_bank(into, left, op, scalar, bank):
             for h in range(2):
                 nc.vector.scalar_tensor_tensor(
-                    halves(into)[:, h, :, :], halves(left)[:, h, :, :], scalar, paired(bank)[:, h, :, :], op, MULT
+                    tile_in_pairs(into)[:, h, :, :], tile_in_pairs(left)[:, h, :, :], scalar,
+                    bank_in_pairs(bank)[:, h, :, :], op, MULT,
                 )
 
         def first_stage(e):
@@ -156,37 +155,35 @@ def tile_moe_rec_glu_sigmoid_kernel(
             a3 = first_product(e, 1, xg, xsg, "w3")
             raw_dh = first_product(e, 2, dyg, dysg, "w2t")
             s = keep.tile([P, H], F32, name="s%d" % e, align_bytes=64)
-            nc.scalar.activation(halves(s[:]), paired(a1), SIGMOID)
+            nc.scalar.activation(tile_in_pairs(s[:]), bank_in_pairs(a1), SIGMOID)
             squares[e] = work.tile([P, H], F32, name="sq")
             nc.scalar.activation(squares[e][:], s[:], SQUARE, bias=-0.5)
             if e > 0:
                 minus_dh[e] = work.tile([P, H], F32, name="minus_dh")
-                nc.scalar.activation(halves(minus_dh[e][:]), paired(raw_dh), COPY, scale=g_neg[:, e : e + 1])
+                nc.scalar.activation(
+                    tile_in_pairs(minus_dh[e][:]), bank_in_pairs(raw_dh), COPY, scale=g_neg[:, e : e + 1]
+                )
             firsts[e] = (a3, raw_dh, s)
-
-        def slope(e):
-            a3, raw_dh, s = firsts[e]
-            sq = squares[e]
-            slopes[e] = work.tile([P, H], F32, name="v")
-            product(slopes[e][:], sq[:], 0.25, a3, SUBTRACT)
 
         def products(e):
             a3, raw_dh, s = firsts[e]
+            v = work.tile([P, H], F32, name="v")
+            times_bank(v[:], squares[e][:], SUBTRACT, 0.25, a3)
             grad = keep.tile([P, 2, H], BF16, name="grad%d" % e, align_bytes=64)
-            product(grad[:, 1, :], s[:], g_col[:, e : e + 1], raw_dh, MULT)
+            times_bank(grad[:, 1, :], s[:], MULT, g_col[:, e : e + 1], raw_dh)
             if e == 0:
-                product(grad[:, 0, :], slopes[e][:], g_neg[:, e : e + 1], raw_dh, MULT)
+                times_bank(grad[:, 0, :], v[:], MULT, g_neg[:, e : e + 1], raw_dh)
             else:
-                nc.gpsimd.tensor_tensor(grad[:, 0, :], minus_dh[e][:], slopes[e][:], MULT)
+                nc.gpsimd.tensor_tensor(grad[:, 0, :], minus_dh[e][:], v[:], MULT)
             gradients[e] = grad
 
         def turn(e):
-            turned = psum.tile([P, 2, 2, C], F32, name=("turned", "turned", "dx0", "dx1")[e])
+            turned = psum.tile([P, 2, 2, C], F32, name="turned" if e < EARLY else "dx%d" % (e - EARLY))
             for j in (1, 0):
                 pairs = gradients[e][:, j, :].bitcast(F32)
                 for h in range(2):
                     nc.tensor.transpose(turned[:, j, h, :], pairs[:, h * P : (h + 1) * P], ident[:])
-            q_ins[e] = keep.tile([P, 2, C * 4], BF16, name=("q_in0", "q_in1", "dx00", "q_in3")[e], align_bytes=64)
+            q_ins[e] = keep.tile([P, 2, C * 4], BF16, name="q_in%d" % e, align_bytes=64)
             nc.scalar.copy(
                 q_ins[e][:].rearrange("p j c -> p (j c)").bitcast(F32).rearrange("p (j c h) -> p j c h", j=2, h=2),
                 turned[:].rearrange("p j h c -> p j c h"),
@@ -202,13 +199,17 @@ def tile_moe_rec_glu_sigmoid_kernel(
 
         dx_banks = (("dx0", "dx1"), ("turned", "first2"), ("first3", "first4"), ("first0", "first1"))
 
-        def second_products(e):
+        def copy_out(e, kt, buffer_name):
+            dx_sb[e, kt] = keep.tile([P, C], F32, name=buffer_name, align_bytes=64)
+            copy = nc.scalar.copy if kt < SCALAR_BLOCKS else nc.vector.tensor_copy
+            copy(dx_sb[e, kt][:], dx_psum[e, kt])
+
+        def second_products(e, left_in_psum=()):
             codes, code_scales = quantised[e]
             for half in ((0, 1) if e == 0 else (1, 0)):
-                copy = nc.vector.tensor_copy if e > 0 and half == 1 else nc.scalar.copy
-                dx = psum.tile([P, 2, C], F32, name=dx_banks[e][half])
-                for b in range(2):
-                    kt = 2 * half + b
+                dx = psum.tile([P, SCALAR_BLOCKS, C], F32, name=dx_banks[e][half])
+                blocks = range(half * SCALAR_BLOCKS, (half + 1) * SCALAR_BLOCKS)
+                for b, kt in enumerate(blocks):
                     for j, n in enumerate(("w1t", "w3t")):
                         nc.tensor.matmul_mx(
                             out=dx[:, b, :],
@@ -218,38 +219,41 @@ def tile_moe_rec_glu_sigmoid_kernel(
                             rhs_scale=code_scales[:, j * C : (j + 1) * C],
                             start=(j == 0), stop=(j == 1),
                         )
-                dx_sb[e, half] = keep.tile([P, 2, C], F32, name="dx%d%d" % (e, half), align_bytes=64)
-                copy(dx_sb[e, half][:], dx[:])
+                    dx_psum[e, kt] = dx[:, b, :]
+                for kt in blocks:
+                    if kt not in left_in_psum:
+                        copy_out(e, kt, "dx%d%d" % (e, kt))
 
         def scatter(e):
             for kt in range(BLOCKS):
                 if e == 0:
                     out_sb[kt] = keep.tile([P, T], F32, name="out%d" % kt)
                 window = out_sb[kt][:].indirect(offsets[:, e * C // 16 : (e + 1) * C // 16])
-                if kt < 2:
-                    nc.scalar.activation(window, dx_sb[e, 0][:, kt, :], COPY)
+                if kt < SCALAR_BLOCKS:
+                    nc.scalar.activation(window, dx_sb[e, kt][:], COPY)
                 else:
-                    nc.vector.tensor_copy(window, dx_sb[e, 1][:, kt - 2, :])
+                    nc.vector.tensor_copy(window, dx_sb[e, kt][:])
                 if e == E - 1:
-                    queue = nc.scalar if kt == 1 else nc.sync
+                    queue = nc.scalar if kt == SCALAR_BLOCKS - 1 else nc.sync
                     queue.dma_start(out[kt * P : (kt + 1) * P, :], out_sb[kt][:])
 
         for e in range(EARLY):
             first_stage(e)
-            slope(e)
             products(e)
         for e in range(EARLY):
             turn(e)
             first_stage(e + EARLY)
             quantise(e)
-            slope(e + EARLY)
             products(e + EARLY)
         second_products(0)
         scatter(0)
+        turn(2)
+        quantise(2)
+        turn(3)
+        second_products(1, left_in_psum=(BLOCKS - 1,))
+        quantise(3)
+        copy_out(1, BLOCKS - 1, "q_in3")
         for e in range(EARLY, E):
-            turn(e)
-            quantise(e)
-            second_products(e - 1)
-        second_products(E - 1)
+            second_products(e)
         for e in range(1, E):
             scatter(e)

@@ -15,16 +15,14 @@ U8 = mybir.dt.uint8
 FP8X4 = mybir.dt.float8_e4m3fn_x4
 FP4X4 = mybir.dt.float4_e2m1fn_x4
 MULT = mybir.AluOpType.mult
+ADD = mybir.AluOpType.add
 SUBTRACT = mybir.AluOpType.subtract
 SIGMOID = mybir.ActivationFunctionType.Sigmoid
-SQUARE = mybir.ActivationFunctionType.Square
 COPY = mybir.ActivationFunctionType.Copy
 
 P = 128
 BLOCKS = K // P
 EARLY = E // 2
-SCALAR_BLOCKS = BLOCKS // 2
-FIRST_BANKS = 5
 
 
 def tile_moe_rec_glu_sigmoid_kernel(
@@ -34,7 +32,6 @@ def tile_moe_rec_glu_sigmoid_kernel(
     nc = tc.nc
     with ExitStack() as ctx:
         keep = ctx.enter_context(tc.tile_pool(name="keep", bufs=1))
-        work = ctx.enter_context(tc.tile_pool(name="work", bufs=E))
         psum = ctx.enter_context(tc.psum_pool(name="psum", bufs=1))
 
         offsets = keep.tile([P, T // 16], U16, name="offsets")
@@ -46,23 +43,26 @@ def tile_moe_rec_glu_sigmoid_kernel(
         words_in = {"w1": w1_words, "w2t": w2t_words, "w3": w3_words, "w1t": w1t_words, "w3t": w3t_words}
         scales_in = {"w1": w1_scales, "w2t": w2t_scales, "w3": w3_scales, "w1t": w1t_scales, "w3t": w3t_scales}
         w = {n: keep.tile([P, E, 1024], U8, name=n + "_w", align_bytes=64) for n in names}
-        ws = {n: keep.tile([P, E, 512], U8, name=n + "_s", align_bytes=64) for n in names}
+        ws = {n: keep.tile([P, E, 512], U8, name=n + "_s", align_bytes=64)[:] for n in names}
+
+        def words(n, e):
+            return w[n][:, e, :]
+
         g_col = keep.tile([P, E], F32, name="g_col")
         g_neg = keep.tile([P, E], F32, name="g_neg")
-        g_rows = keep.tile([P, C], F32, name="g_rows")
         ident = keep.tile([P, P], F32, name="ident")
 
         def zero(tile):
             nc.vector.memset(tile.bitcast(I32), 0)
 
         def zero_plane(n):
-            zero(ws[n][:].rearrange("p e c -> p (e c)"))
+            zero(ws[n].rearrange("p e c -> p (e c)"))
 
         zero(xs_win[:])
         zero_plane("w1")
         zero(dys_win[:])
-        for n in ("w3", "w2t"):
-            zero_plane(n)
+        zero_plane("w2t")
+        zero_plane("w3")
 
         def load_token_scales(tile, src):
             for r in range(4):
@@ -80,12 +80,11 @@ def tile_moe_rec_glu_sigmoid_kernel(
                 w[n][:, lo:hi, :].bitcast(I32), words_in[n][lo:hi, 0, :, :].rearrange("e p c -> p e c").bitcast(I32)
             )
 
-        for n in ("w3", "w2t"):
+        for n in ("w1", "w2t", "w3"):
             load_words(nc.gpsimd, n, 0, EARLY)
-        nc.gpsimd.memset(g_rows[:], 0.0)
         make_identity(nc, ident[:])
         for n in ("w1t", "w3t"):
-            nc.gpsimd.memset(ws[n][:].rearrange("p e c -> p (e c)").bitcast(I32), 0)
+            nc.gpsimd.memset(ws[n].rearrange("p e c -> p (e c)").bitcast(I32), 0)
         for n in ("w1t", "w3t"):
             load_words(nc.gpsimd, n, 0, EARLY)
 
@@ -93,23 +92,18 @@ def tile_moe_rec_glu_sigmoid_kernel(
         nc.sync.dma_start(x_win[:], x_words[0].rearrange("p t d -> p (t d)").bitcast(I32))
         load_token_scales(xs_win, x_scales)
         nc.sync.dma_start(dy_win[:], dy_words[0].rearrange("p t d -> p (t d)").bitcast(I32))
-        load_words(nc.sync, "w1", 0, EARLY)
         load_weight_scales("w1")
         load_token_scales(dys_win, dy_scales)
-        for n in ("w3", "w2t"):
-            load_weight_scales(n)
-        nc.sync.dma_start(g_rows[0:E, :], gate[0, :].rearrange("(e u) -> e u", e=E))
-        for n in ("w1", "w3", "w2t"):
+        load_weight_scales("w2t")
+        with nc.allow_non_contiguous_dma(reason="one gate value a slot and partition"):
+            nc.sync.dma_start(g_col[:], gate[0, :].rearrange("(e u) -> u e", e=E))
+        load_weight_scales("w3")
+        for n in ("w1", "w2t", "w3"):
             load_words(nc.sync, n, EARLY, E)
         for n in ("w1t", "w3t"):
             load_weight_scales(n)
         for n in ("w1t", "w3t"):
             load_words(nc.sync, n, EARLY, E)
-
-        g_turned = psum.tile([P, BLOCKS, C], F32, name="dx1")
-        nc.tensor.transpose(g_turned[:, 0, :], g_rows[:], ident[:])
-        nc.scalar.copy(g_col[:], g_turned[:, 0, 0:E])
-        nc.scalar.activation(g_neg[:], g_turned[:, 0, 0:E], COPY, scale=-1.0)
 
         xg = keep.tile([P, T], U32, name="xg", align_bytes=64)
         dyg = keep.tile([P, T], U32, name="dyg", align_bytes=64)
@@ -124,136 +118,176 @@ def tile_moe_rec_glu_sigmoid_kernel(
         for into, window in zip((xg, xsg, dyg, dysg), windows):
             for half in range(2):
                 gather(into, window, half)
+        nc.scalar.activation(g_neg[:], g_col[:], COPY, scale=-1.0)
 
-        squares, minus_dh, firsts, gradients = {}, {}, {}, {}
-        q_ins, quantised, dx_psum, dx_sb, out_sb = {}, {}, {}, {}, {}
+        def bank(b, shape):
+            return psum.tile(shape, F32, name="bank%d" % b)
 
-        def first_product(e, place, codes, code_scales, n):
-            bank = psum.tile([P, H], F32, name="first%d" % ((3 * e + place) % FIRST_BANKS))
+        def first_product(e, b, codes, code_scales, n):
+            acc = bank(b, [P, H])
             cols = slice(e * C, (e + 1) * C)
             nc.tensor.matmul_mx(
-                out=bank[:], lhsT=codes[:, cols].bitcast(FP8X4), lhsT_scale=code_scales[:, cols],
-                rhs=w[n][:, e, :].bitcast(FP4X4), rhs_scale=ws[n][:, e, :], start=True, stop=True,
+                out=acc[:], lhsT=codes[:, cols].bitcast(FP8X4), lhsT_scale=code_scales[:, cols],
+                rhs=words(n, e).bitcast(FP4X4), rhs_scale=ws[n][:, e, :], start=True, stop=True,
             )
-            return bank
+            return acc[:].rearrange("q (p h d) -> q h p d", h=2, d=2)
 
-        def bank_in_pairs(bank):
-            return bank[:].rearrange("q (p h d) -> q h p d", h=2, d=2)
+        def in_pairs(tile):
+            return tile[:].rearrange("q (h p d) -> q h p d", h=2, d=2)
 
-        def tile_in_pairs(values):
-            return values.rearrange("q (h p d) -> q h p d", h=2, d=2)
-
-        def times_bank(into, left, op, scalar, bank):
+        def times_bank(into, left, op, scalar, values):
             for h in range(2):
                 nc.vector.scalar_tensor_tensor(
-                    tile_in_pairs(into)[:, h, :, :], tile_in_pairs(left)[:, h, :, :], scalar,
-                    bank_in_pairs(bank)[:, h, :, :], op, MULT,
+                    in_pairs(into)[:, h, :, :], in_pairs(left)[:, h, :, :], scalar, values[:, h, :, :], op, MULT
                 )
 
-        def first_stage(e):
-            a1 = first_product(e, 0, xg, xsg, "w1")
-            a3 = first_product(e, 1, xg, xsg, "w3")
-            raw_dh = first_product(e, 2, dyg, dysg, "w2t")
-            s = keep.tile([P, H], F32, name="s%d" % e, align_bytes=64)
-            nc.scalar.activation(tile_in_pairs(s[:]), bank_in_pairs(a1), SIGMOID)
-            squares[e] = work.tile([P, H], F32, name="sq")
-            nc.scalar.activation(squares[e][:], s[:], SQUARE, bias=-0.5)
-            if e > 0:
-                minus_dh[e] = work.tile([P, H], F32, name="minus_dh")
-                nc.scalar.activation(
-                    tile_in_pairs(minus_dh[e][:]), bank_in_pairs(raw_dh), COPY, scale=g_neg[:, e : e + 1]
-                )
-            firsts[e] = (a3, raw_dh, s)
+        s, u, t, da1, q_in, codes, code_scales, dx, dx_sb, out_sb = {}, {}, {}, {}, {}, {}, {}, {}, {}, {}
 
-        def products(e):
-            a3, raw_dh, s = firsts[e]
-            v = work.tile([P, H], F32, name="v")
-            times_bank(v[:], squares[e][:], SUBTRACT, 0.25, a3)
-            grad = keep.tile([P, 2, H], BF16, name="grad%d" % e, align_bytes=64)
-            times_bank(grad[:, 1, :], s[:], MULT, g_col[:, e : e + 1], raw_dh)
-            if e == 0:
-                times_bank(grad[:, 0, :], v[:], MULT, g_neg[:, e : e + 1], raw_dh)
-            else:
-                nc.gpsimd.tensor_tensor(grad[:, 0, :], minus_dh[e][:], v[:], MULT)
-            gradients[e] = grad
+        def sigmoid(e, b):
+            a1 = first_product(e, b, xg, xsg, "w1")
+            s[e] = keep.tile([P, H], F32, name="s%d" % e, align_bytes=64)
+            nc.scalar.activation(in_pairs(s[e]), a1, SIGMOID)
 
-        def turn(e):
-            turned = psum.tile([P, 2, 2, C], F32, name="turned" if e < EARLY else "dx%d" % (e - EARLY))
-            for j in (1, 0):
-                pairs = gradients[e][:, j, :].bitcast(F32)
-                for h in range(2):
-                    nc.tensor.transpose(turned[:, j, h, :], pairs[:, h * P : (h + 1) * P], ident[:])
-            q_ins[e] = keep.tile([P, 2, C * 4], BF16, name="q_in%d" % e, align_bytes=64)
+        def slope(e, b):
+            a3 = first_product(e, b, xg, xsg, "w3")
+            u[e] = keep.tile([P, H], F32, name="u%d" % e, align_bytes=64)
+            times_bank(u[e], s[e], SUBTRACT, 1.0, a3)
+
+        def gated(e, b):
+            dh = first_product(e, b, dyg, dysg, "w2t")
+            t[e] = keep.tile([P, H], F32, name="t%d" % e)
+            times_bank(t[e], s[e], MULT, g_neg[:, e : e + 1], dh)
+
+        def product(e):
+            da1[e] = keep.tile([P, H], BF16, name="da1_%d" % e, align_bytes=64)
+            engine = nc.vector if e == 0 else nc.gpsimd
+            engine.tensor_tensor(da1[e][:], t[e][:], u[e][:], MULT)
+
+        def turn3(e, b):
+            turned = bank(b, [P, 4, C])
+            for h in range(2):
+                for d in range(2):
+                    nc.tensor.transpose(turned[:, 2 * h + d, :], in_pairs(t[e])[:, h, :, d], ident[:])
+            q_in[e] = keep.tile([P, 2, C * 4], BF16, name="q_in%d" % e, align_bytes=64)
+            nc.scalar.activation(
+                q_in[e][:, 1, :].rearrange("p (c d) -> p c d", d=4), turned[:].rearrange("p d c -> p c d"),
+                COPY, scale=-1.0,
+            )
+
+        def turn1(e, b):
+            turned = bank(b, [P, 2, C])
+            pairs = da1[e][:].bitcast(F32)
+            for h in range(2):
+                nc.tensor.transpose(turned[:, h, :], pairs[:, h * P : (h + 1) * P], ident[:])
             nc.scalar.copy(
-                q_ins[e][:].rearrange("p j c -> p (j c)").bitcast(F32).rearrange("p (j c h) -> p j c h", j=2, h=2),
-                turned[:].rearrange("p j h c -> p j c h"),
+                q_in[e][:, 0, :].bitcast(F32).rearrange("p (c h) -> p c h", h=2), turned[:].rearrange("p h c -> p c h")
             )
 
         def quantise(e):
-            codes = work.tile([P, 2 * C], U32, name="codes", align_bytes=64)
-            code_scales = work.tile([P, 2 * C], U8, name="code_scales", align_bytes=64)
+            codes[e] = keep.tile([P, 2 * C], U32, name="codes%d" % e, align_bytes=64)
+            code_scales[e] = keep.tile([P, 2 * C], U8, name="code_scales%d" % e, align_bytes=64)
             nc.vector.quantize_mx(
-                out=codes[:].bitcast(FP8X4), scales=code_scales[:], in_=q_ins[e][:].rearrange("p j c -> p (j c)")
+                out=codes[e][:].bitcast(FP8X4), scales=code_scales[e][:], in_=q_in[e][:].rearrange("p j c -> p (j c)")
             )
-            quantised[e] = (codes, code_scales)
 
-        dx_banks = (("dx0", "dx1"), ("turned", "first2"), ("first3", "first4"), ("first0", "first1"))
+        late = {kt: keep.tile([P, (E - 1) * C], F32, name="late%d" % kt) for kt in (1, 3)}
 
-        def copy_out(e, kt, buffer_name):
-            dx_sb[e, kt] = keep.tile([P, C], F32, name=buffer_name, align_bytes=64)
-            copy = nc.scalar.copy if kt < SCALAR_BLOCKS else nc.vector.tensor_copy
-            copy(dx_sb[e, kt][:], dx_psum[e, kt])
+        def row_block(e, kt, acc):
+            for j, n in enumerate(("w1t", "w3t")):
+                nc.tensor.matmul_mx(
+                    out=acc,
+                    lhsT=words(n, e)[:, 2 * P * kt : 2 * P * (kt + 1)].bitcast(FP4X4),
+                    lhsT_scale=ws[n][:, e, P * kt : P * (kt + 1)],
+                    rhs=codes[e][:, j * C : (j + 1) * C].bitcast(FP8X4),
+                    rhs_scale=code_scales[e][:, j * C : (j + 1) * C],
+                    start=(j == 0), stop=(j == 1),
+                )
 
-        def second_products(e, left_in_psum=()):
-            codes, code_scales = quantised[e]
-            for half in ((0, 1) if e == 0 else (1, 0)):
-                dx = psum.tile([P, SCALAR_BLOCKS, C], F32, name=dx_banks[e][half])
-                blocks = range(half * SCALAR_BLOCKS, (half + 1) * SCALAR_BLOCKS)
-                for b, kt in enumerate(blocks):
-                    for j, n in enumerate(("w1t", "w3t")):
-                        nc.tensor.matmul_mx(
-                            out=dx[:, b, :],
-                            lhsT=w[n][:, e, 2 * P * kt : 2 * P * (kt + 1)].bitcast(FP4X4),
-                            lhsT_scale=ws[n][:, e, P * kt : P * (kt + 1)],
-                            rhs=codes[:, j * C : (j + 1) * C].bitcast(FP8X4),
-                            rhs_scale=code_scales[:, j * C : (j + 1) * C],
-                            start=(j == 0), stop=(j == 1),
-                        )
-                    dx_psum[e, kt] = dx[:, b, :]
-                for kt in blocks:
-                    if kt not in left_in_psum:
-                        copy_out(e, kt, "dx%d%d" % (e, kt))
+        def copy_out(e, kt, acc, copy):
+            if kt % 2 == 1 and e > 0:
+                dx_sb[e, kt] = late[kt][:, (e - 1) * C : e * C]
+            else:
+                name = "q_in3" if (e, kt) == (2, 2) else "dx%d%d" % (e, kt)
+                dx_sb[e, kt] = keep.tile([P, C], F32, name=name, align_bytes=64)[:]
+            copy(dx_sb[e, kt], acc)
 
-        def scatter(e):
-            for kt in range(BLOCKS):
-                if e == 0:
-                    out_sb[kt] = keep.tile([P, T], F32, name="out%d" % kt)
-                window = out_sb[kt][:].indirect(offsets[:, e * C // 16 : (e + 1) * C // 16])
-                if kt < SCALAR_BLOCKS:
-                    nc.scalar.activation(window, dx_sb[e, kt][:], COPY)
-                else:
-                    nc.vector.tensor_copy(window, dx_sb[e, kt][:])
-                if e == E - 1:
-                    queue = nc.scalar if kt == SCALAR_BLOCKS - 1 else nc.sync
-                    queue.dma_start(out[kt * P : (kt + 1) * P, :], out_sb[kt][:])
+        def second(e, half, b):
+            acc = bank(b, [P, 2, C])
+            for place in range(2):
+                row_block(e, 2 * half + place, acc[:, place, :])
+            for place in range(2):
+                copy_out(e, 2 * half + place, acc[:, place, :], nc.scalar.copy if half == 0 else nc.vector.tensor_copy)
 
-        for e in range(EARLY):
-            first_stage(e)
-            products(e)
-        for e in range(EARLY):
-            turn(e)
-            first_stage(e + EARLY)
-            quantise(e)
-            products(e + EARLY)
-        second_products(0)
-        scatter(0)
-        turn(2)
+        def second_of_first_expert(banks):
+            for blocks, b in banks:
+                acc = bank(b, [P, len(blocks), C])
+                for place, kt in enumerate(blocks):
+                    row_block(0, kt, acc[:, place, :])
+                for place, kt in enumerate(blocks):
+                    copy_out(0, kt, acc[:, place, :], nc.scalar.copy)
+
+        out_buffers = ("out0", "da1_3", "out2", "q_in3")
+
+        def scatter(kt, values, lo, hi):
+            if kt not in out_sb:
+                out_sb[kt] = keep.tile([P, T], F32, name=out_buffers[kt], align_bytes=64)
+            window = out_sb[kt][:].indirect(offsets[:, lo * C // 16 : hi * C // 16])
+            if kt < 2:
+                nc.scalar.activation(window, values, COPY)
+            else:
+                nc.vector.tensor_copy(window, values)
+
+        def store(kt, queue):
+            queue.dma_start(out[kt * P : (kt + 1) * P, :], out_sb[kt][:])
+
+        sigmoid(0, 0)
+        sigmoid(1, 1)
+        gated(0, 2)
+        gated(1, 3)
+        slope(0, 4)
+        product(0)
+        slope(1, 5)
+        product(1)
+        sigmoid(2, 0)
+        turn3(0, 4)
+        turn1(0, 6)
+        quantise(0)
+        sigmoid(3, 4)
+        gated(2, 2)
+        slope(2, 3)
+        product(2)
+        turn3(1, 5)
+        second_of_first_expert((((0,), 6), ((2,), 0), ((1, 3), 2)))
+        turn1(1, 6)
+        gated(3, 1)
+        slope(3, 7)
+        product(3)
+        quantise(1)
+        turn3(2, 0)
+        turn1(2, 2)
         quantise(2)
-        turn(3)
-        second_products(1, left_in_psum=(BLOCKS - 1,))
+        turn3(3, 6)
+        second(1, 1, 5)
+        second(1, 0, 3)
+        turn1(3, 0)
         quantise(3)
-        copy_out(1, BLOCKS - 1, "q_in3")
-        for e in range(EARLY, E):
-            second_products(e)
-        for e in range(1, E):
-            scatter(e)
+        for kt in (0, 2):
+            scatter(kt, dx_sb[0, kt], 0, 1)
+        second(2, 1, 4)
+        second(2, 0, 0)
+        for kt in (0, 2):
+            scatter(kt, dx_sb[1, kt], 1, 2)
+        scatter(1, dx_sb[0, 1], 0, 1)
+        for kt in (0, 2):
+            scatter(kt, dx_sb[2, kt], 2, 3)
+        scatter(3, dx_sb[0, 3], 0, 1)
+        second(3, 1, 1)
+        second(3, 0, 7)
+        for kt in (0, 2):
+            scatter(kt, dx_sb[3, kt], 3, 4)
+        for kt in (0, 2):
+            store(kt, nc.sync)
+        for kt in (1, 3):
+            scatter(kt, late[kt][:], 1, E)
+        store(3, nc.sync)
+        store(1, nc.scalar)

@@ -48,7 +48,7 @@ def tile_moe_rec_glu_sigmoid_kernel(
         def words(n, e):
             return w[n][:, e, :]
 
-        g_col = keep.tile([P, E], F32, name="g_col")
+        g_rows = keep.tile([P, C], F32, name="g_rows")
         g_neg = keep.tile([P, E], F32, name="g_neg")
         ident = keep.tile([P, P], F32, name="ident")
 
@@ -80,9 +80,9 @@ def tile_moe_rec_glu_sigmoid_kernel(
                 w[n][:, lo:hi, :].bitcast(I32), words_in[n][lo:hi, 0, :, :].rearrange("e p c -> p e c").bitcast(I32)
             )
 
+        make_identity(nc, ident[:])
         for n in ("w1", "w2t", "w3"):
             load_words(nc.gpsimd, n, 0, EARLY)
-        make_identity(nc, ident[:])
         for n in ("w1t", "w3t"):
             nc.gpsimd.memset(ws[n].rearrange("p e c -> p (e c)").bitcast(I32), 0)
         for n in ("w1t", "w3t"):
@@ -92,11 +92,10 @@ def tile_moe_rec_glu_sigmoid_kernel(
         nc.sync.dma_start(x_win[:], x_words[0].rearrange("p t d -> p (t d)").bitcast(I32))
         load_token_scales(xs_win, x_scales)
         nc.sync.dma_start(dy_win[:], dy_words[0].rearrange("p t d -> p (t d)").bitcast(I32))
+        nc.sync.dma_start(g_rows[:], gate[0 : P // E, :].rearrange("r (e u) -> (r e) u", e=E))
         load_weight_scales("w1")
         load_token_scales(dys_win, dy_scales)
         load_weight_scales("w2t")
-        with nc.allow_non_contiguous_dma(reason="one gate value a slot and partition"):
-            nc.sync.dma_start(g_col[:], gate[0, :].rearrange("(e u) -> u e", e=E))
         load_weight_scales("w3")
         for n in ("w1", "w2t", "w3"):
             load_words(nc.sync, n, EARLY, E)
@@ -118,10 +117,13 @@ def tile_moe_rec_glu_sigmoid_kernel(
         for into, window in zip((xg, xsg, dyg, dysg), windows):
             for half in range(2):
                 gather(into, window, half)
-        nc.scalar.activation(g_neg[:], g_col[:], COPY, scale=-1.0)
 
         def bank(b, shape):
             return psum.tile(shape, F32, name="bank%d" % b)
+
+        g_turned = bank(7, [P, P])
+        nc.tensor.transpose(g_turned[:], g_rows[:], ident[:])
+        nc.vector.tensor_scalar(g_neg[:], g_turned[:, 0:E], -1.0, None, MULT)
 
         def first_product(e, b, codes, code_scales, n):
             acc = bank(b, [P, H])
@@ -130,23 +132,20 @@ def tile_moe_rec_glu_sigmoid_kernel(
                 out=acc[:], lhsT=codes[:, cols].bitcast(FP8X4), lhsT_scale=code_scales[:, cols],
                 rhs=words(n, e).bitcast(FP4X4), rhs_scale=ws[n][:, e, :], start=True, stop=True,
             )
-            return acc[:].rearrange("q (p h d) -> q h p d", h=2, d=2)
+            return acc[:].rearrange("q (p d) -> q d p", d=4)
 
-        def in_pairs(tile):
-            return tile[:].rearrange("q (h p d) -> q h p d", h=2, d=2)
+        def planes(tile):
+            return tile[:].rearrange("q (d p) -> q d p", d=4)
 
         def times_bank(into, left, op, scalar, values):
-            for h in range(2):
-                nc.vector.scalar_tensor_tensor(
-                    in_pairs(into)[:, h, :, :], in_pairs(left)[:, h, :, :], scalar, values[:, h, :, :], op, MULT
-                )
+            nc.vector.scalar_tensor_tensor(planes(into), planes(left), scalar, values, op, MULT)
 
         s, u, t, da1, q_in, codes, code_scales, dx, dx_sb, out_sb = {}, {}, {}, {}, {}, {}, {}, {}, {}, {}
 
         def sigmoid(e, b):
             a1 = first_product(e, b, xg, xsg, "w1")
             s[e] = keep.tile([P, H], F32, name="s%d" % e, align_bytes=64)
-            nc.scalar.activation(in_pairs(s[e]), a1, SIGMOID)
+            nc.scalar.activation(planes(s[e]), a1, SIGMOID)
 
         def slope(e, b):
             a3 = first_product(e, b, xg, xsg, "w3")
@@ -161,13 +160,17 @@ def tile_moe_rec_glu_sigmoid_kernel(
         def product(e):
             da1[e] = keep.tile([P, H], BF16, name="da1_%d" % e, align_bytes=64)
             engine = nc.vector if e == 0 else nc.gpsimd
-            engine.tensor_tensor(da1[e][:], t[e][:], u[e][:], MULT)
+            engine.tensor_tensor(
+                da1[e][:].rearrange("q (h p b) -> q h p b", h=2, b=2),
+                t[e][:].rearrange("q (h b p) -> q h p b", h=2, b=2),
+                u[e][:].rearrange("q (h b p) -> q h p b", h=2, b=2),
+                MULT,
+            )
 
         def turn3(e, b):
             turned = bank(b, [P, 4, C])
-            for h in range(2):
-                for d in range(2):
-                    nc.tensor.transpose(turned[:, 2 * h + d, :], in_pairs(t[e])[:, h, :, d], ident[:])
+            for d in range(4):
+                nc.tensor.transpose(turned[:, d, :], planes(t[e])[:, d, :], ident[:])
             q_in[e] = keep.tile([P, 2, C * 4], BF16, name="q_in%d" % e, align_bytes=64)
             nc.scalar.activation(
                 q_in[e][:, 1, :].rearrange("p (c d) -> p c d", d=4), turned[:].rearrange("p d c -> p c d"),

@@ -158,8 +158,8 @@ def tile_moe_rec_glu_sigmoid_kernel(
             times_bank(t[e], s[e], MULT, g_neg[:, e : e + 1], dh)
 
         def product(e):
-            da1[e] = keep.tile([P, H], BF16, name="da1_%d" % e, align_bytes=64)
-            engine = nc.vector if e == 0 else nc.gpsimd
+            da1[e] = keep.tile([P, H], BF16, name="q_in1" if e == E - 1 else "da1_%d" % e, align_bytes=64)
+            engine = nc.vector if e in (0, E - 1) else nc.gpsimd
             engine.tensor_tensor(
                 da1[e][:].rearrange("q (h p b) -> q h p b", h=2, b=2),
                 t[e][:].rearrange("q (h b p) -> q h p b", h=2, b=2),
@@ -229,7 +229,7 @@ def tile_moe_rec_glu_sigmoid_kernel(
                 for place, kt in enumerate(blocks):
                     copy_out(0, kt, acc[:, place, :], nc.scalar.copy)
 
-        out_buffers = ("out0", "da1_3", "out2", "q_in3")
+        out_buffers = ("out0", "q_in1", "out2", "out3")
 
         def scatter(kt, values, lo, hi):
             if kt not in out_sb:
@@ -264,8 +264,8 @@ def tile_moe_rec_glu_sigmoid_kernel(
         turn1(1, 6)
         gated(3, 1)
         slope(3, 7)
-        product(3)
         quantise(1)
+        product(3)
         turn3(2, 0)
         turn1(2, 2)
         quantise(2)

@@ -158,7 +158,7 @@ def tile_moe_rec_glu_sigmoid_kernel(
             times_bank(t[e], s[e], MULT, g_neg[:, e : e + 1], dh)
 
         def product(e):
-            da1[e] = keep.tile([P, H], BF16, name="q_in1" if e == E - 1 else "da1_%d" % e, align_bytes=64)
+            da1[e] = keep.tile([P, H], BF16, name={2: "q_in0", 3: "q_in1"}.get(e, "da1_%d" % e), align_bytes=64)
             engine = nc.vector if e in (0, E - 1) else nc.gpsimd
             engine.tensor_tensor(
                 da1[e][:].rearrange("q (h p b) -> q h p b", h=2, b=2),

from contextlib import ExitStack

import concourse.mybir as mybir
from concourse.masks import make_identity

K, T, E, C, H, N = 512, 512, 4, 128, 512, 512
FLOPS = 5 * 2 * 512 * 512 * 512

F32 = mybir.dt.float32
BF16 = mybir.dt.bfloat16
I32 = mybir.dt.int32
U32 = mybir.dt.uint32
U16 = mybir.dt.uint16
U8 = mybir.dt.uint8
FP8X4 = mybir.dt.float8_e4m3fn_x4
FP4X4 = mybir.dt.float4_e2m1fn_x4
MULT = mybir.AluOpType.mult
ADD = mybir.AluOpType.add
SUBTRACT = mybir.AluOpType.subtract
SIGMOID = mybir.ActivationFunctionType.Sigmoid
COPY = mybir.ActivationFunctionType.Copy

P = 128
BLOCKS = K // P
EARLY = E // 2


def tile_moe_rec_glu_sigmoid_kernel(
    tc, x_words, x_scales, dy_words, dy_scales, w1_words, w1_scales, w3_words, w3_scales,
    w2t_words, w2t_scales, w1t_words, w1t_scales, w3t_words, w3t_scales, gate, offs, out,
):
    nc = tc.nc
    with ExitStack() as ctx:
        keep = ctx.enter_context(tc.tile_pool(name="keep", bufs=1))
        psum = ctx.enter_context(tc.psum_pool(name="psum", bufs=1))

        offsets = keep.tile([P, T // 16], U16, name="offsets")
        x_win = keep.tile([P, T], I32, name="x_win", align_bytes=64)
        dy_win = keep.tile([P, T], I32, name="dy_win", align_bytes=64)
        xs_win = keep.tile([P, T], U8, name="xs_win", align_bytes=64)
        dys_win = keep.tile([P, T], U8, name="dys_win", align_bytes=64)
        names = ("w1", "w2t", "w3", "w1t", "w3t")
        words_in = {"w1": w1_words, "w2t": w2t_words, "w3": w3_words, "w1t": w1t_words, "w3t": w3t_words}
        scales_in = {"w1": w1_scales, "w2t": w2t_scales, "w3": w3_scales, "w1t": w1t_scales, "w3t": w3t_scales}
        w = {n: keep.tile([P, E, 1024], U8, name=n + "_w", align_bytes=64) for n in names}
        ws = {n: keep.tile([P, E, 512], U8, name=n + "_s", align_bytes=64)[:] for n in names}

        def words(n, e):
            return w[n][:, e, :]

        g_rows = keep.tile([P, C], F32, name="g_rows")
        g_neg = keep.tile([P, E], F32, name="g_neg")
        ident = keep.tile([P, P], F32, name="ident")

        def zero(tile):
            nc.vector.memset(tile.bitcast(I32), 0)

        def zero_plane(n):
            zero(ws[n].rearrange("p e c -> p (e c)"))

        zero(xs_win[:])
        zero_plane("w1")
        zero(dys_win[:])
        zero_plane("w2t")
        zero_plane("w3")

        def load_token_scales(tile, src):
            for r in range(4):
                nc.sync.dma_start(tile[r:P:32, :].bitcast(I32), src[0, r:16:4, :].bitcast(I32))

        def load_weight_scales(n):
            for r in range(4):
                nc.sync.dma_start(
                    ws[n][r:P:32, :, :].bitcast(I32),
                    scales_in[n][:, 0, r:16:4, :].rearrange("e b c -> b e c").bitcast(I32),
                )

        def load_words(queue, n, lo, hi):
            queue.dma_start(
                w[n][:, lo:hi, :].bitcast(I32), words_in[n][lo:hi, 0, :, :].rearrange("e p c -> p e c").bitcast(I32)
            )

        make_identity(nc, ident[:])
        for n in ("w1", "w2t", "w3"):
            load_words(nc.gpsimd, n, 0, EARLY)
        for n in ("w1t", "w3t"):
            nc.gpsimd.memset(ws[n].rearrange("p e c -> p (e c)").bitcast(I32), 0)
        for n in ("w1t", "w3t"):
            load_words(nc.gpsimd, n, 0, EARLY)

        nc.sync.dma_start(offsets[:], offs)
        nc.sync.dma_start(x_win[:], x_words[0].rearrange("p t d -> p (t d)").bitcast(I32))
        load_token_scales(xs_win, x_scales)
        nc.sync.dma_start(dy_win[:], dy_words[0].rearrange("p t d -> p (t d)").bitcast(I32))
        nc.sync.dma_start(g_rows[:], gate[0 : P // E, :].rearrange("r (e u) -> (r e) u", e=E))
        load_weight_scales("w1")
        load_token_scales(dys_win, dy_scales)
        load_weight_scales("w2t")
        load_weight_scales("w3")
        for n in ("w1", "w2t", "w3"):
            load_words(nc.sync, n, EARLY, E)
        for n in ("w1t", "w3t"):
            load_weight_scales(n)
        for n in ("w1t", "w3t"):
            load_words(nc.sync, n, EARLY, E)

        xg = keep.tile([P, T], U32, name="xg", align_bytes=64)
        dyg = keep.tile([P, T], U32, name="dyg", align_bytes=64)
        xsg = keep.tile([P, T], U8, name="xsg", align_bytes=64)
        dysg = keep.tile([P, T], U8, name="dysg", align_bytes=64)

        def gather(into, window, half):
            lo, hi = half * T // 2, (half + 1) * T // 2
            nc.vector.tensor_copy(into[:, lo:hi], window.indirect(offsets[:, lo // 16 : hi // 16]))

        windows = (x_win[:].bitcast(U32), xs_win[:], dy_win[:].bitcast(U32), dys_win[:])
        for into, window in zip((xg, xsg, dyg, dysg), windows):
            for half in range(2):
                gather(into, window, half)

        def bank(b, shape):
            return psum.tile(shape, F32, name="bank%d" % b)

        g_turned = bank(7, [P, P])
        nc.tensor.transpose(g_turned[:], g_rows[:], ident[:])
        nc.vector.tensor_scalar(g_neg[:], g_turned[:, 0:E], -1.0, None, MULT)

        def first_product(e, b, codes, code_scales, n):
            acc = bank(b, [P, H])
            cols = slice(e * C, (e + 1) * C)
            nc.tensor.matmul_mx(
                out=acc[:], lhsT=codes[:, cols].bitcast(FP8X4), lhsT_scale=code_scales[:, cols],
                rhs=words(n, e).bitcast(FP4X4), rhs_scale=ws[n][:, e, :], start=True, stop=True,
            )
            return acc[:].rearrange("q (p d) -> q d p", d=4)

        def planes(tile):
            return tile[:].rearrange("q (d p) -> q d p", d=4)

        def times_bank(into, left, op, scalar, values):
            nc.vector.scalar_tensor_tensor(planes(into), planes(left), scalar, values, op, MULT)

        s, u, t, da1, q_in, codes, code_scales, dx, dx_sb, out_sb = {}, {}, {}, {}, {}, {}, {}, {}, {}, {}

        def sigmoid(e, b):
            a1 = first_product(e, b, xg, xsg, "w1")
            s[e] = keep.tile([P, H], F32, name="s%d" % e, align_bytes=64)
            nc.scalar.activation(planes(s[e]), a1, SIGMOID)

        def slope(e, b):
            a3 = first_product(e, b, xg, xsg, "w3")
            u[e] = keep.tile([P, H], F32, name="u%d" % e, align_bytes=64)
            times_bank(u[e], s[e], SUBTRACT, 1.0, a3)

        def gated(e, b):
            dh = first_product(e, b, dyg, dysg, "w2t")
            t[e] = keep.tile([P, H], F32, name="t%d" % e)
            times_bank(t[e], s[e], MULT, g_neg[:, e : e + 1], dh)

        def product(e):
            da1[e] = keep.tile([P, H], BF16, name={2: "q_in0", 3: "q_in1"}.get(e, "da1_%d" % e), align_bytes=64)
            engine = nc.vector if e in (0, E - 1) else nc.gpsimd
            engine.tensor_tensor(
                da1[e][:].rearrange("q (h p b) -> q h p b", h=2, b=2),
                t[e][:].rearrange("q (h b p) -> q h p b", h=2, b=2),
                u[e][:].rearrange("q (h b p) -> q h p b", h=2, b=2),
                MULT,
            )

        def turn3(e, b):
            turned = bank(b, [P, 4, C])
            for d in range(4):
                nc.tensor.transpose(turned[:, d, :], planes(t[e])[:, d, :], ident[:])
            q_in[e] = keep.tile([P, 2, C * 4], BF16, name="q_in%d" % e, align_bytes=64)
            nc.scalar.activation(
                q_in[e][:, 1, :].rearrange("p (c d) -> p c d", d=4), turned[:].rearrange("p d c -> p c d"),
                COPY, scale=-1.0,
            )

        def turn1(e, b):
            turned = bank(b, [P, 2, C])
            pairs = da1[e][:].bitcast(F32)
            for h in range(2):
                nc.tensor.transpose(turned[:, h, :], pairs[:, h * P : (h + 1) * P], ident[:])
            nc.scalar.copy(
                q_in[e][:, 0, :].bitcast(F32).rearrange("p (c h) -> p c h", h=2), turned[:].rearrange("p h c -> p c h")
            )

        def quantise(e):
            codes[e] = keep.tile([P, 2 * C], U32, name="codes%d" % e, align_bytes=64)
            code_scales[e] = keep.tile([P, 2 * C], U8, name="code_scales%d" % e, align_bytes=64)
            nc.vector.quantize_mx(
                out=codes[e][:].bitcast(FP8X4), scales=code_scales[e][:], in_=q_in[e][:].rearrange("p j c -> p (j c)")
            )

        late = {kt: keep.tile([P, (E - 1) * C], F32, name="late%d" % kt) for kt in (1, 3)}

        def row_block(e, kt, acc):
            for j, n in enumerate(("w1t", "w3t")):
                nc.tensor.matmul_mx(
                    out=acc,
                    lhsT=words(n, e)[:, 2 * P * kt : 2 * P * (kt + 1)].bitcast(FP4X4),
                    lhsT_scale=ws[n][:, e, P * kt : P * (kt + 1)],
                    rhs=codes[e][:, j * C : (j + 1) * C].bitcast(FP8X4),
                    rhs_scale=code_scales[e][:, j * C : (j + 1) * C],
                    start=(j == 0), stop=(j == 1),
                )

        def copy_out(e, kt, acc, copy):
            if kt % 2 == 1 and e > 0:
                dx_sb[e, kt] = late[kt][:, (e - 1) * C : e * C]
            else:
                name = "q_in3" if (e, kt) == (2, 2) else "dx%d%d" % (e, kt)
                dx_sb[e, kt] = keep.tile([P, C], F32, name=name, align_bytes=64)[:]
            copy(dx_sb[e, kt], acc)

        def second(e, half, b):
            acc = bank(b, [P, 2, C])
            for place in range(2):
                row_block(e, 2 * half + place, acc[:, place, :])
            for place in range(2):
                copy_out(e, 2 * half + place, acc[:, place, :], nc.scalar.copy if half == 0 else nc.vector.tensor_copy)

        def second_of_first_expert(banks):
            for blocks, b in banks:
                acc = bank(b, [P, len(blocks), C])
                for place, kt in enumerate(blocks):
                    row_block(0, kt, acc[:, place, :])
                for place, kt in enumerate(blocks):
                    copy_out(0, kt, acc[:, place, :], nc.scalar.copy)

        out_buffers = ("out0", "q_in1", "out2", "out3")

        def scatter(kt, values, lo, hi):
            if kt not in out_sb:
                out_sb[kt] = keep.tile([P, T], F32, name=out_buffers[kt], align_bytes=64)
            window = out_sb[kt][:].indirect(offsets[:, lo * C // 16 : hi * C // 16])
            if kt < 2:
                nc.scalar.activation(window, values, COPY)
            else:
                nc.vector.tensor_copy(window, values)

        def store(kt, queue):
            queue.dma_start(out[kt * P : (kt + 1) * P, :], out_sb[kt][:])

        sigmoid(0, 0)
        sigmoid(1, 1)
        gated(0, 2)
        gated(1, 3)
        slope(0, 4)
        product(0)
        slope(1, 5)
        product(1)
        sigmoid(2, 0)
        turn3(0, 4)
        turn1(0, 6)
        quantise(0)
        sigmoid(3, 4)
        gated(2, 2)
        slope(2, 3)
        product(2)
        turn3(1, 5)
        second_of_first_expert((((0,), 6), ((2,), 0), ((1, 3), 2)))
        turn1(1, 6)
        gated(3, 1)
        slope(3, 7)
        quantise(1)
        product(3)
        turn3(2, 0)
        turn1(2, 2)
        quantise(2)
        turn3(3, 6)
        second(1, 1, 5)
        second(1, 0, 3)
        turn1(3, 0)
        quantise(3)
        for kt in (0, 2):
            scatter(kt, dx_sb[0, kt], 0, 1)
        second(2, 1, 4)
        second(2, 0, 0)
        for kt in (0, 2):
            scatter(kt, dx_sb[1, kt], 1, 2)
        scatter(1, dx_sb[0, 1], 0, 1)
        for kt in (0, 2):
            scatter(kt, dx_sb[2, kt], 2, 3)
        scatter(3, dx_sb[0, 3], 0, 1)
        second(3, 1, 1)
        second(3, 0, 7)
        for kt in (0, 2):
            scatter(kt, dx_sb[3, kt], 3, 4)
        for kt in (0, 2):
            store(kt, nc.sync)
        for kt in (1, 3):
            scatter(kt, late[kt][:], 1, E)
        store(3, nc.sync)
        store(1, nc.scalar)
